import numpy as np
import ml_dtypes


def mxq(x, axis, fmt="e4m3"):
    dtype, down = {"e4m3": (ml_dtypes.float8_e4m3fn, 7), "e5m2": (ml_dtypes.float8_e5m2, 14)}[fmt]
    v = np.moveaxis(np.asarray(x, np.float32).astype(ml_dtypes.bfloat16).astype(np.float64), axis, -1)
    blocks = v.reshape(v.shape[:-1] + (-1, 32))
    amax = np.abs(blocks).max(-1, keepdims=True)
    byte = np.maximum(np.where(amax > 0, np.frexp(amax)[1] - 1 + 127, 0) - down, 1)
    scale = np.exp2(byte - 127.0)
    codes = (blocks / scale).astype(np.float32).astype(dtype).astype(np.float64)
    return np.moveaxis((codes * scale).reshape(v.shape), -1, axis)


WIDE = False


def mx_kscale(k):
    if not WIDE:
        return np.ones(k)
    levels = np.array([10, -10, 5, -5, 0])
    if k % 512:
        return np.exp2(np.random.permutation(np.resize(levels, k // 32))).repeat(32)
    a = np.empty((k // 512, 16))
    for p in range(k // 512):
        a[p, :8] = np.random.permutation(np.resize(levels, 8))
        for g in range(8):
            far = levels[np.abs(levels - a[p, g]) >= 10]
            a[p, g + 8] = far[np.random.randint(len(far))]
    return np.exp2(a.ravel()).repeat(32)


def f64(x):
    return np.asarray(x).astype(np.float64)


def striped(idx):
    return np.tile(idx.reshape(-1, 16).T, (8, 1)).astype(np.uint16)


def unstriped(offs):
    return offs[:16].T.reshape(-1).astype(np.int64)


def silu(v):
    return v / (1.0 + np.exp(-np.maximum(v, -700.0)))


K, T, D, S, V, N = 1024, 2048, 16, 512, 32, 512


def setup_inputs():
    n = np.random.standard_normal
    s = mx_kscale(K)[:, None]
    return {
        "xT": (n((K, T)) * s).astype(np.float32),
        "w": (n((K, N)) / np.sqrt(K) / s).astype(np.float32),
        "b": (0.3 * n((N, 1))).astype(np.float32),
        "offs": striped(np.random.permutation(T)[:S]),
    }


def reference(xT, w, b, offs):
    idx = unstriped(offs)
    xq = mxq(f64(xT)[:, idx], 0, "e4m3")
    y = mxq(f64(w), 0, "e4m3").T @ xq
    y = silu(y + f64(b))
    return y.reshape(N, V, D).max(axis=2)

@@ -1,0 +1,199 @@
+from contextlib import ExitStack
+
+import concourse.mybir as mybir
+from concourse.masks import make_identity
+
+K, T, D, S, V, N = 1024, 2048, 16, 512, 32, 512
+FLOPS = 2 * K * N * S
+
+F32 = mybir.dt.float32
+BF16 = mybir.dt.bfloat16
+U32 = mybir.dt.uint32
+U16 = mybir.dt.uint16
+U8 = mybir.dt.uint8
+FP8X4 = mybir.dt.float8_e4m3fn_x4
+SILU = mybir.ActivationFunctionType.Silu
+AX = mybir.AxisListType.X
+MAX = mybir.AluOpType.max
+
+P = 128
+PACK = 4
+K_PASS = P * PACK
+PASSES = K // K_PASS
+M_TILES = N // P
+HALF = S // 2
+HALVED = (0, 3)
+
+LOADS = (
+    [("x", 0, 0, 1, 0), ("x", 0, 1, 2, 1), ("x", 0, 2, 3, 0), ("x", 0, 3, 4, 1)]
+    + [("x", 1, 0, 1, 0), ("x", 1, 1, 2, 1), ("x", 1, 2, 3, 0)]
+    + [("w", 0, 0, 512, 1)]
+    + [("x", 1, 3, 4, 0), ("w", 1, 0, 256, 0), ("w", 1, 256, 128, 0), ("w", 1, 384, 128, 0)]
+)
+
+
+def token_parts(m):
+    return [(0, HALF), (HALF, S)] if m in HALVED else [(0, S)]
+
+
+def tile_picked_pool_lin_silu_sub_e_kernel(tc, xT, w, b, offs, out):
+    nc = tc.nc
+    with ExitStack() as ctx:
+        keep = ctx.enter_context(tc.tile_pool(name="keep", bufs=1))
+        psum = ctx.enter_context(tc.psum_pool(name="psum", bufs=1))
+
+        offsets = keep.tile([P, S // 16], U16, name="offsets")
+        nc.sync.dma_start(offsets[:], offs)
+
+        b_rows = keep.tile([P, P], F32, name="b_rows")
+        nc.gpsimd.memset(b_rows[:], 0.0)
+        nc.gpsimd.dma_start(out=b_rows[0:M_TILES, :], in_=b.rearrange("(t p) o -> t (p o)", t=M_TILES))
+
+        queues = (nc.sync, nc.scalar)
+        planes = {}
+        raws = {}
+        for item in LOADS:
+            a = item[1]
+            rows = slice(a * K_PASS, (a + 1) * K_PASS)
+            if item[0] == "x":
+                j0, j1 = item[2], item[3]
+                table = keep.tile([P, j1 - j0, T], F32, name=f"table_{a}_{j0}")
+                queues[item[4]].dma_start(out=table[:], in_=xT[rows, :].rearrange("(p j) t -> p j t", j=PACK)[:, j0:j1, :])
+                for j in range(j0, j1):
+                    planes[(a, j)] = table[:, j - j0, :]
+            else:
+                c, width = item[2], item[3]
+                raw = keep.tile([P, PACK, width], F32, name=f"raw_{a}_{c}")
+                queues[item[4]].dma_start(out=raw[:], in_=w[rows, c : c + width].rearrange("(p j) n -> p j n", j=PACK))
+                raws[(a, c)] = raw
+
+        warm = keep.tile([P, 1], F32, name="warm")
+        warm_out = keep.tile([P, 1], F32, name="warm_out")
+        nc.vector.memset(warm[:], 0.0)
+        nc.scalar.activation(warm_out[:], warm[:], SILU)
+
+        ident = keep.tile([P, P], F32, name="ident")
+        bias = keep.tile([P, M_TILES], F32, name="bias")
+        make_identity(nc, ident[:])
+        b_cols = psum.tile([P, P], F32, name="b_cols")
+        nc.tensor.transpose(b_cols[:], b_rows[:], ident[:])
+        nc.vector.tensor_copy(bias[:], b_cols[:, 0:M_TILES])
+
+        x_grouped = []
+        x_codes = []
+        x_scales = []
+        for a in range(PASSES):
+            xg = keep.tile([P, S, PACK], BF16, align_bytes=64, name=f"xg_{a}")
+            xc = keep.tile([P, S], U32, align_bytes=64, name=f"xc_{a}")
+            xs = keep.tile([P, S], U8, align_bytes=64, name=f"xs_{a}")
+            x_grouped.append(xg)
+            x_codes.append(xc)
+            x_scales.append(xs)
+
+        def gather(a, j, n0, n1):
+            nc.vector.tensor_copy(
+                out=x_grouped[a][:, n0:n1, j],
+                in_=planes[(a, j)].indirect(offsets[:, n0 // 16 : n1 // 16]),
+            )
+
+        def quantize_x(a, n0, n1):
+            nc.vector.quantize_mx(
+                out=x_codes[a][:, n0:n1].bitcast(FP8X4),
+                scales=x_scales[a][:, n0:n1],
+                in_=x_grouped[a][:, n0:n1, :].rearrange("p n j -> p (n j)"),
+            )
+
+        w_grouped = []
+        w_codes = []
+        w_scales = []
+        for a in range(PASSES):
+            wg = keep.tile([P, N, PACK], BF16, align_bytes=64, name=f"wg_{a}")
+            wc = keep.tile([P, N], U32, align_bytes=64, name=f"wc_{a}")
+            ws = keep.tile([P, N], U8, align_bytes=64, name=f"ws_{a}")
+            w_grouped.append(wg)
+            w_codes.append(wc)
+            w_scales.append(ws)
+
+        def interleave_w(copy, a, c0, c1):
+            for (pass_, first), raw in raws.items():
+                if pass_ == a and first <= c0 and c1 <= first + raw.shape[2]:
+                    copy(
+                        w_grouped[a][:, c0:c1, :].rearrange("p (c i) j -> p c j i", i=4),
+                        raw[:, :, c0 - first : c1 - first].rearrange("p j (c i) -> p c j i", i=4),
+                    )
+
+        def quantize_w(a, c0, c1):
+            nc.vector.quantize_mx(
+                out=w_codes[a][:, c0:c1].bitcast(FP8X4),
+                scales=w_scales[a][:, c0:c1],
+                in_=w_grouped[a][:, c0:c1, :].rearrange("p n j -> p (n j)"),
+            )
+
+        acc = {}
+        for m in range(M_TILES):
+            for n0, n1 in token_parts(m):
+                bank = psum.tile([P, n1 - n0], F32, name=f"acc_{m}_{n0}")
+                acc[(m, n0)] = bank
+
+        pooled = keep.tile([P, M_TILES, V], F32, name="pooled")
+
+        def multiply(a, m, parts=None):
+            for n0, n1 in parts or token_parts(m):
+                nc.tensor.matmul_mx(
+                    out=acc[(m, n0)][:],
+                    lhsT=w_codes[a][:, m * P : (m + 1) * P].bitcast(FP8X4),
+                    lhsT_scale=w_scales[a][:, m * P : (m + 1) * P],
+                    rhs=x_codes[a][:, n0:n1].bitcast(FP8X4),
+                    rhs_scale=x_scales[a][:, n0:n1],
+                    start=(a == 0),
+                    stop=(a == PASSES - 1),
+                )
+
+        def finish(m, parts=None):
+            for n0, n1 in parts or token_parts(m):
+                y = keep.tile([P, n1 - n0], F32, name=f"y_{m}_{n0}")
+                nc.scalar.activation(y[:], acc[(m, n0)][:], SILU, bias=bias[:, m : m + 1])
+                nc.vector.tensor_reduce(
+                    out=pooled[:, m, n0 // D : n1 // D], in_=y[:].rearrange("p (v d) -> p v d", d=D), axis=AX, op=MAX
+                )
+
+        s_copy = nc.scalar.copy
+        v_copy = nc.vector.tensor_copy
+        out_view = out.rearrange("(t p) v -> p t v", p=P)
+
+        gather(0, 0, 0, S)
+        gather(0, 1, 0, S)
+        gather(0, 2, 0, S)
+        gather(0, 3, 0, S)
+        interleave_w(s_copy, 0, 0, N)
+        quantize_x(0, 0, S)
+        gather(1, 0, 0, S)
+        quantize_w(0, 0, N)
+        for m in range(M_TILES):
+            multiply(0, m)
+        gather(1, 1, 0, S)
+        gather(1, 2, 0, S)
+        gather(1, 3, 0, HALF)
+        gather(1, 3, HALF, S)
+        interleave_w(s_copy, 1, 0, 128)
+        interleave_w(s_copy, 1, 128, 256)
+        quantize_x(1, 0, HALF)
+        quantize_w(1, 0, 128)
+        multiply(1, 0, [(0, HALF)])
+        finish(0, [(0, HALF)])
+        quantize_x(1, HALF, S)
+        multiply(1, 0, [(HALF, S)])
+        finish(0, [(HALF, S)])
+        quantize_w(1, 128, 256)
+        multiply(1, 1)
+        interleave_w(v_copy, 1, 256, 384)
+        quantize_w(1, 256, 384)
+        multiply(1, 2)
+        finish(1)
+        interleave_w(v_copy, 1, 384, 512)
+        quantize_w(1, 384, 512)
+        multiply(1, 3)
+        finish(2)
+        nc.sync.dma_start(out=out_view[:, 0 : M_TILES - 1, :], in_=pooled[:, 0 : M_TILES - 1, :])
+        finish(3)
+        nc.sync.dma_start(out=out_view[:, M_TILES - 1, :], in_=pooled[:, M_TILES - 1, :])

@@ -24,12 +24,10 @@ M_TILES = N // P
 HALF = S // 2
 HALVED = (0, 3)
 
-LOADS = (
-    [("x", 0, 0, 1, 0), ("x", 0, 1, 2, 1), ("x", 0, 2, 3, 0), ("x", 0, 3, 4, 1)]
-    + [("x", 1, 0, 1, 0), ("x", 1, 1, 2, 1), ("x", 1, 2, 3, 0)]
-    + [("w", 0, 0, 512, 1)]
-    + [("x", 1, 3, 4, 0), ("w", 1, 0, 256, 0), ("w", 1, 256, 128, 0), ("w", 1, 384, 128, 0)]
-)
+PLANES = [(0, 0), (0, 1), (0, 2), (1, 0), (1, 1), (1, 2), (0, 3), (1, 3)]
+EARLY = 2
+LAST = M_TILES - 1
+PIECES = [(a, m) for m in range(M_TILES) for a in range(PASSES) if a > 0 or m >= EARLY]
 
 
 def token_parts(m):
@@ -39,33 +37,38 @@ def token_parts(m):
 def tile_picked_pool_lin_silu_sub_e_kernel(tc, xT, w, b, offs, out):
     nc = tc.nc
     with ExitStack() as ctx:
+        lists = ctx.enter_context(tc.tile_pool(name="lists", bufs=1))
         keep = ctx.enter_context(tc.tile_pool(name="keep", bufs=1))
+        late = ctx.enter_context(tc.tile_pool(name="late", bufs=1))
         psum = ctx.enter_context(tc.psum_pool(name="psum", bufs=1))
-
-        offsets = keep.tile([P, S // 16], U16, name="offsets")
-        nc.sync.dma_start(offsets[:], offs)
 
         b_rows = keep.tile([P, P], F32, name="b_rows")
         nc.gpsimd.memset(b_rows[:], 0.0)
-        nc.gpsimd.dma_start(out=b_rows[0:M_TILES, :], in_=b.rearrange("(t p) o -> t (p o)", t=M_TILES))
+        nc.scalar.dma_start(out=b_rows[0:M_TILES, :], in_=b.rearrange("(t p) o -> t (p o)", t=M_TILES))
 
-        queues = (nc.sync, nc.scalar)
-        planes = {}
+        def pass_rows(tensor, a):
+            return tensor[a * K_PASS : (a + 1) * K_PASS, :].rearrange("(p j) n -> p j n", j=PACK)
+
         raws = {}
-        for item in LOADS:
-            a = item[1]
-            rows = slice(a * K_PASS, (a + 1) * K_PASS)
-            if item[0] == "x":
-                j0, j1 = item[2], item[3]
-                table = keep.tile([P, j1 - j0, T], F32, name=f"table_{a}_{j0}")
-                queues[item[4]].dma_start(out=table[:], in_=xT[rows, :].rearrange("(p j) t -> p j t", j=PACK)[:, j0:j1, :])
-                for j in range(j0, j1):
-                    planes[(a, j)] = table[:, j - j0, :]
+
+        def load_w(a, c, width):
+            raw = keep.tile([P, PACK, width], F32, align_bytes=64, name=f"raw_{a}_{c}", tag=f"raw_{a}_{c}")
+            nc.sync.dma_start(out=raw[:], in_=pass_rows(w, a)[:, :, c : c + width])
+            raws[(a, c)] = raw
+
+        load_w(0, 0, EARLY * P)
+        offsets = lists.tile([P, S // 16], U16, name="offsets")
+        nc.sync.dma_start(offsets[:], offs)
+        planes = {}
+        for a, j in PLANES:
+            if (a, j) == PLANES[-1]:
+                plane = late.tile([P, T], F32, align_bytes=64, offset=0, name="last_plane")
             else:
-                c, width = item[2], item[3]
-                raw = keep.tile([P, PACK, width], F32, name=f"raw_{a}_{c}")
-                queues[item[4]].dma_start(out=raw[:], in_=w[rows, c : c + width].rearrange("(p j) n -> p j n", j=PACK))
-                raws[(a, c)] = raw
+                plane = keep.tile([P, T], F32, align_bytes=64, name=f"plane_{a}_{j}")
+            nc.sync.dma_start(out=plane[:], in_=pass_rows(xT, a)[:, j, :])
+            planes[(a, j)] = plane
+        for a, m in PIECES:
+            load_w(a, m * P, P)
 
         warm = keep.tile([P, 1], F32, name="warm")
         warm_out = keep.tile([P, 1], F32, name="warm_out")
@@ -77,23 +80,16 @@ def tile_picked_pool_lin_silu_sub_e_kernel(tc, xT, w, b, offs, out):
         make_identity(nc, ident[:])
         b_cols = psum.tile([P, P], F32, name="b_cols")
         nc.tensor.transpose(b_cols[:], b_rows[:], ident[:])
-        nc.vector.tensor_copy(bias[:], b_cols[:, 0:M_TILES])
+        nc.scalar.copy(bias[:], b_cols[:, 0:M_TILES])
 
-        x_grouped = []
-        x_codes = []
-        x_scales = []
-        for a in range(PASSES):
-            xg = keep.tile([P, S, PACK], BF16, align_bytes=64, name=f"xg_{a}")
-            xc = keep.tile([P, S], U32, align_bytes=64, name=f"xc_{a}")
-            xs = keep.tile([P, S], U8, align_bytes=64, name=f"xs_{a}")
-            x_grouped.append(xg)
-            x_codes.append(xc)
-            x_scales.append(xs)
+        x_grouped = [keep.tile([P, S, PACK], BF16, align_bytes=64, name=f"xg_{a}") for a in range(PASSES)]
+        x_codes = [keep.tile([P, S], U32, align_bytes=64, name=f"xc_{a}") for a in range(PASSES)]
+        x_scales = [keep.tile([P, S], U8, align_bytes=64, name=f"xs_{a}") for a in range(PASSES)]
 
         def gather(a, j, n0, n1):
             nc.vector.tensor_copy(
                 out=x_grouped[a][:, n0:n1, j],
-                in_=planes[(a, j)].indirect(offsets[:, n0 // 16 : n1 // 16]),
+                in_=planes[(a, j)][:].indirect(offsets[:, n0 // 16 : n1 // 16]),
             )
 
         def quantize_x(a, n0, n1):
@@ -103,97 +99,110 @@ def tile_picked_pool_lin_silu_sub_e_kernel(tc, xT, w, b, offs, out):
                 in_=x_grouped[a][:, n0:n1, :].rearrange("p n j -> p (n j)"),
             )
 
-        w_grouped = []
-        w_codes = []
-        w_scales = []
-        for a in range(PASSES):
-            wg = keep.tile([P, N, PACK], BF16, align_bytes=64, name=f"wg_{a}")
-            wc = keep.tile([P, N], U32, align_bytes=64, name=f"wc_{a}")
-            ws = keep.tile([P, N], U8, align_bytes=64, name=f"ws_{a}")
-            w_grouped.append(wg)
-            w_codes.append(wc)
-            w_scales.append(ws)
+        w_codes, w_scales, w_grouped = {}, {}, {}
 
-        def interleave_w(copy, a, c0, c1):
-            for (pass_, first), raw in raws.items():
-                if pass_ == a and first <= c0 and c1 <= first + raw.shape[2]:
-                    copy(
-                        w_grouped[a][:, c0:c1, :].rearrange("p (c i) j -> p c j i", i=4),
-                        raw[:, :, c0 - first : c1 - first].rearrange("p j (c i) -> p c j i", i=4),
-                    )
-
-        def quantize_w(a, c0, c1):
-            nc.vector.quantize_mx(
-                out=w_codes[a][:, c0:c1].bitcast(FP8X4),
-                scales=w_scales[a][:, c0:c1],
-                in_=w_grouped[a][:, c0:c1, :].rearrange("p n j -> p (n j)"),
+        def interleave(a, m, width, copy, place=None):
+            if place is None:
+                w_grouped[(a, m)] = keep.tile([P, width, PACK], BF16, align_bytes=64, name=f"wg_{a}_{m}")
+            else:
+                w_grouped[(a, m)] = late.tile([P, width, PACK], BF16, align_bytes=64, offset=place, name=f"wg_{a}_{m}")
+            copy(
+                w_grouped[(a, m)][:].rearrange("p (c i) j -> p c j i", i=4),
+                raws[(a, m * P)][:].rearrange("p j (c i) -> p c j i", i=4),
             )
+
+        def quantize_w(a, m, width, place=None):
+            if place is None:
+                codes = keep.tile([P, width], U32, align_bytes=64, name=f"wc_{a}_{m}")
+            else:
+                codes = late.tile([P, width], U32, align_bytes=64, offset=place, name=f"wc_{a}_{m}")
+            scales = keep.tile([P, width], U8, align_bytes=64, name=f"ws_{a}_{m}")
+            nc.vector.quantize_mx(
+                out=codes[:].bitcast(FP8X4), scales=scales[:], in_=w_grouped[(a, m)][:].rearrange("p n j -> p (n j)")
+            )
+            for u in range(width // P):
+                w_codes[(a, m + u)] = codes[:, u * P : (u + 1) * P]
+                w_scales[(a, m + u)] = scales[:, u * P : (u + 1) * P]
+
+        def quantize_late(a, m):
+            quantize_w(a, m, P, place=4 * P * PIECES.index((a, m)))
+
+        def interleave_late(a, m):
+            if m == LAST:
+                interleave(a, m, P, nc.vector.tensor_copy, place=4096 + 2 * P * PACK * a)
+            else:
+                interleave(a, m, P, nc.scalar.copy)
 
         acc = {}
         for m in range(M_TILES):
             for n0, n1 in token_parts(m):
-                bank = psum.tile([P, n1 - n0], F32, name=f"acc_{m}_{n0}")
-                acc[(m, n0)] = bank
-
-        pooled = keep.tile([P, M_TILES, V], F32, name="pooled")
+                acc[(m, n0)] = psum.tile([P, n1 - n0], F32, name=f"acc_{m}_{n0}")
 
         def multiply(a, m, parts=None):
             for n0, n1 in parts or token_parts(m):
                 nc.tensor.matmul_mx(
                     out=acc[(m, n0)][:],
-                    lhsT=w_codes[a][:, m * P : (m + 1) * P].bitcast(FP8X4),
-                    lhsT_scale=w_scales[a][:, m * P : (m + 1) * P],
+                    lhsT=w_codes[(a, m)].bitcast(FP8X4),
+                    lhsT_scale=w_scales[(a, m)],
                     rhs=x_codes[a][:, n0:n1].bitcast(FP8X4),
                     rhs_scale=x_scales[a][:, n0:n1],
                     start=(a == 0),
                     stop=(a == PASSES - 1),
                 )
 
-        def finish(m, parts=None):
+        def activate(m):
+            for n0, n1 in token_parts(m):
+                nc.scalar.activation(y[:, m, n0:n1], acc[(m, n0)][:], SILU, bias=bias[:, m : m + 1])
+
+        def pool_max(m, parts=None):
             for n0, n1 in parts or token_parts(m):
-                y = keep.tile([P, n1 - n0], F32, name=f"y_{m}_{n0}")
-                nc.scalar.activation(y[:], acc[(m, n0)][:], SILU, bias=bias[:, m : m + 1])
                 nc.vector.tensor_reduce(
-                    out=pooled[:, m, n0 // D : n1 // D], in_=y[:].rearrange("p (v d) -> p v d", d=D), axis=AX, op=MAX
+                    out=pooled[:, m, n0 // D : n1 // D],
+                    in_=y[:, m, n0:n1].rearrange("p (v d) -> p v d", d=D),
+                    axis=AX,
+                    op=MAX,
                 )
 
-        s_copy = nc.scalar.copy
-        v_copy = nc.vector.tensor_copy
         out_view = out.rearrange("(t p) v -> p t v", p=P)
 
+        interleave(0, 0, EARLY * P, nc.scalar.copy)
         gather(0, 0, 0, S)
-        gather(0, 1, 0, S)
-        gather(0, 2, 0, S)
-        gather(0, 3, 0, S)
-        interleave_w(s_copy, 0, 0, N)
+        quantize_w(0, 0, EARLY * P)
+        for a, j in PLANES[1:-1]:
+            gather(a, j, 0, S)
         quantize_x(0, 0, S)
-        gather(1, 0, 0, S)
-        quantize_w(0, 0, N)
-        for m in range(M_TILES):
+        for m in range(EARLY):
             multiply(0, m)
-        gather(1, 1, 0, S)
-        gather(1, 2, 0, S)
         gather(1, 3, 0, HALF)
         gather(1, 3, HALF, S)
-        interleave_w(s_copy, 1, 0, 128)
-        interleave_w(s_copy, 1, 128, 256)
+        for a, m in PIECES[:-2]:
+            interleave_late(a, m)
         quantize_x(1, 0, HALF)
-        quantize_w(1, 0, 128)
+        quantize_late(1, 0)
         multiply(1, 0, [(0, HALF)])
-        finish(0, [(0, HALF)])
         quantize_x(1, HALF, S)
         multiply(1, 0, [(HALF, S)])
-        finish(0, [(HALF, S)])
-        quantize_w(1, 128, 256)
+        quantize_late(1, 1)
         multiply(1, 1)
-        interleave_w(v_copy, 1, 256, 384)
-        quantize_w(1, 256, 384)
+        quantize_late(0, 2)
+        multiply(0, 2)
+        interleave_late(0, LAST)
+        quantize_late(1, 2)
         multiply(1, 2)
-        finish(1)
-        interleave_w(v_copy, 1, 384, 512)
-        quantize_w(1, 384, 512)
-        multiply(1, 3)
-        finish(2)
-        nc.sync.dma_start(out=out_view[:, 0 : M_TILES - 1, :], in_=pooled[:, 0 : M_TILES - 1, :])
-        finish(3)
-        nc.sync.dma_start(out=out_view[:, M_TILES - 1, :], in_=pooled[:, M_TILES - 1, :])
+        quantize_late(0, LAST)
+        multiply(0, LAST)
+        interleave_late(1, LAST)
+        y = keep.tile([P, M_TILES, S], F32, align_bytes=64, name="y", tag=f"raw_1_{(LAST - 1) * P}")
+        for m in range(LAST):
+            activate(m)
+        pooled = keep.tile([P, M_TILES, V], F32, align_bytes=64, name="pooled", tag=f"raw_1_{LAST * P}")
+        pool_max(0, [(0, HALF)])
+        quantize_late(1, LAST)
+        multiply(1, LAST)
+        activate(LAST)
+        pool_max(0, [(HALF, S)])
+        for m in range(1, LAST):
+            pool_max(m)
+        nc.sync.dma_start(out=out_view[:, 0:LAST, :], in_=pooled[:, 0:LAST, :])
+        pool_max(LAST)
+        nc.sync.dma_start(out=out_view[:, LAST, :], in_=pooled[:, LAST, :])

@@ -24,14 +24,16 @@ M_TILES = N // P
 HALF = S // 2
 HALVED = (0, 3)
 
-PLANES = [(0, 0), (0, 1), (0, 2), (1, 0), (1, 1), (1, 2), (0, 3), (1, 3)]
-EARLY = 2
 LAST = M_TILES - 1
-PIECES = [(a, m) for m in range(M_TILES) for a in range(PASSES) if a > 0 or m >= EARLY]
+LAST_PLANE = (PASSES - 1, PACK - 1)
+FIRST_HALF, SECOND_HALF = [(0, HALF)], [(HALF, S)]
+EARLY = 2
+X_LOADS = [(0, 0, 1), (0, 1, 1), (0, 2, 1), (1, 0, 1), (1, 1, 1), (1, 2, 1), (0, 3, 1), (1, 3, 1)]
+PIECES = [(0, 2), (1, 0), (1, 1), (1, 2), (0, 3), (1, 3)]
 
 
 def token_parts(m):
-    return [(0, HALF), (HALF, S)] if m in HALVED else [(0, S)]
+    return FIRST_HALF + SECOND_HALF if m in HALVED else [(0, S)]
 
 
 def tile_picked_pool_lin_silu_sub_e_kernel(tc, xT, w, b, offs, out):
@@ -51,24 +53,31 @@ def tile_picked_pool_lin_silu_sub_e_kernel(tc, xT, w, b, offs, out):
 
         raws = {}
 
-        def load_w(a, c, width):
-            raw = keep.tile([P, PACK, width], F32, align_bytes=64, name=f"raw_{a}_{c}", tag=f"raw_{a}_{c}")
-            nc.sync.dma_start(out=raw[:], in_=pass_rows(w, a)[:, :, c : c + width])
-            raws[(a, c)] = raw
+        def load_w(a, m, tiles=1):
+            raw = keep.tile([P, PACK, tiles * P], F32, align_bytes=64, name=f"raw_{a}_{m}", tag=f"raw_{a}_{m}")
+            nc.sync.dma_start(out=raw[:], in_=pass_rows(w, a)[:, :, m * P : (m + tiles) * P])
+            raws[(a, m)] = raw
 
-        load_w(0, 0, EARLY * P)
-        offsets = lists.tile([P, S // 16], U16, name="offsets")
-        nc.sync.dma_start(offsets[:], offs)
         planes = {}
-        for a, j in PLANES:
-            if (a, j) == PLANES[-1]:
-                plane = late.tile([P, T], F32, align_bytes=64, offset=0, name="last_plane")
+
+        def load_x(a, j, count=1):
+            if (a, j) == LAST_PLANE:
+                table = late.tile([P, T], F32, align_bytes=64, offset=0, name="last_plane")
+                nc.sync.dma_start(out=table[:], in_=pass_rows(xT, a)[:, j, :])
+                planes[(a, j)] = table[:]
             else:
-                plane = keep.tile([P, T], F32, align_bytes=64, name=f"plane_{a}_{j}")
-            nc.sync.dma_start(out=plane[:], in_=pass_rows(xT, a)[:, j, :])
-            planes[(a, j)] = plane
+                table = keep.tile([P, count, T], F32, align_bytes=64, name=f"planes_{a}_{j}")
+                nc.sync.dma_start(out=table[:], in_=pass_rows(xT, a)[:, j : j + count, :])
+                for u in range(count):
+                    planes[(a, j + u)] = table[:, u, :]
+
+        offsets = lists.tile([P, S // 16], U16, name="offsets")
+        load_w(0, 0, EARLY)
+        nc.sync.dma_start(offsets[:], offs)
+        for a, j, count in X_LOADS:
+            load_x(a, j, count)
         for a, m in PIECES:
-            load_w(a, m * P, P)
+            load_w(a, m)
 
         warm = keep.tile([P, 1], F32, name="warm")
         warm_out = keep.tile([P, 1], F32, name="warm_out")
@@ -86,52 +95,43 @@ def tile_picked_pool_lin_silu_sub_e_kernel(tc, xT, w, b, offs, out):
         x_codes = [keep.tile([P, S], U32, align_bytes=64, name=f"xc_{a}") for a in range(PASSES)]
         x_scales = [keep.tile([P, S], U8, align_bytes=64, name=f"xs_{a}") for a in range(PASSES)]
 
-        def gather(a, j, n0, n1):
+        def gather(a, j, n0=0, n1=S):
             nc.vector.tensor_copy(
                 out=x_grouped[a][:, n0:n1, j],
-                in_=planes[(a, j)][:].indirect(offsets[:, n0 // 16 : n1 // 16]),
+                in_=planes[(a, j)].indirect(offsets[:, n0 // 16 : n1 // 16]),
             )
 
-        def quantize_x(a, n0, n1):
+        def quantize_x(a, n0=0, n1=S):
             nc.vector.quantize_mx(
                 out=x_codes[a][:, n0:n1].bitcast(FP8X4),
                 scales=x_scales[a][:, n0:n1],
                 in_=x_grouped[a][:, n0:n1, :].rearrange("p n j -> p (n j)"),
             )
 
-        w_codes, w_scales, w_grouped = {}, {}, {}
-
-        def interleave(a, m, width, copy, place=None):
+        def w_tile(m, dtype, columns, place, name):
             if place is None:
-                w_grouped[(a, m)] = keep.tile([P, width, PACK], BF16, align_bytes=64, name=f"wg_{a}_{m}")
-            else:
-                w_grouped[(a, m)] = late.tile([P, width, PACK], BF16, align_bytes=64, offset=place, name=f"wg_{a}_{m}")
-            copy(
-                w_grouped[(a, m)][:].rearrange("p (c i) j -> p c j i", i=4),
-                raws[(a, m * P)][:].rearrange("p j (c i) -> p c j i", i=4),
-            )
+                return keep.tile([P, columns], dtype, align_bytes=64, name=name)
+            return late.tile([P, columns], dtype, align_bytes=64, offset=place, name=name)
 
-        def quantize_w(a, m, width, place=None):
-            if place is None:
-                codes = keep.tile([P, width], U32, align_bytes=64, name=f"wc_{a}_{m}")
-            else:
-                codes = late.tile([P, width], U32, align_bytes=64, offset=place, name=f"wc_{a}_{m}")
-            scales = keep.tile([P, width], U8, align_bytes=64, name=f"ws_{a}_{m}")
+        w_grouped = [w_tile(m, BF16, PASSES * P * PACK, None if m < LAST else 4096, f"wg_{m}") for m in range(M_TILES)]
+        w_codes = [w_tile(m, U32, PASSES * P, None if m < EARLY else 1024 * m, f"wc_{m}") for m in range(M_TILES)]
+        w_scales = [keep.tile([P, PASSES * P], U8, align_bytes=64, name=f"ws_{m}") for m in range(M_TILES)]
+
+        def interleave(copy, a, m, c0=0, c1=P):
+            for (pass_, first), raw in raws.items():
+                if pass_ == a and first <= m < first + raw.shape[2] // P:
+                    base = (m - first) * P
+                    copy(
+                        w_grouped[m][:, (a * P + c0) * PACK : (a * P + c1) * PACK].rearrange("p (c i j) -> p c j i", i=4, j=PACK),
+                        raw[:, :, base + c0 : base + c1].rearrange("p j (c i) -> p c j i", i=4),
+                    )
+
+        def quantize_w(m, a0=0, a1=PASSES):
             nc.vector.quantize_mx(
-                out=codes[:].bitcast(FP8X4), scales=scales[:], in_=w_grouped[(a, m)][:].rearrange("p n j -> p (n j)")
+                out=w_codes[m][:, a0 * P : a1 * P].bitcast(FP8X4),
+                scales=w_scales[m][:, a0 * P : a1 * P],
+                in_=w_grouped[m][:, a0 * P * PACK : a1 * P * PACK],
             )
-            for u in range(width // P):
-                w_codes[(a, m + u)] = codes[:, u * P : (u + 1) * P]
-                w_scales[(a, m + u)] = scales[:, u * P : (u + 1) * P]
-
-        def quantize_late(a, m):
-            quantize_w(a, m, P, place=4 * P * PIECES.index((a, m)))
-
-        def interleave_late(a, m):
-            if m == LAST:
-                interleave(a, m, P, nc.vector.tensor_copy, place=4096 + 2 * P * PACK * a)
-            else:
-                interleave(a, m, P, nc.scalar.copy)
 
         acc = {}
         for m in range(M_TILES):
@@ -142,19 +142,19 @@ def tile_picked_pool_lin_silu_sub_e_kernel(tc, xT, w, b, offs, out):
             for n0, n1 in parts or token_parts(m):
                 nc.tensor.matmul_mx(
                     out=acc[(m, n0)][:],
-                    lhsT=w_codes[(a, m)].bitcast(FP8X4),
-                    lhsT_scale=w_scales[(a, m)],
+                    lhsT=w_codes[m][:, a * P : (a + 1) * P].bitcast(FP8X4),
+                    lhsT_scale=w_scales[m][:, a * P : (a + 1) * P],
                     rhs=x_codes[a][:, n0:n1].bitcast(FP8X4),
                     rhs_scale=x_scales[a][:, n0:n1],
                     start=(a == 0),
                     stop=(a == PASSES - 1),
                 )
 
-        def activate(m):
-            for n0, n1 in token_parts(m):
+        def activate(y, m, parts=None):
+            for n0, n1 in parts or token_parts(m):
                 nc.scalar.activation(y[:, m, n0:n1], acc[(m, n0)][:], SILU, bias=bias[:, m : m + 1])
 
-        def pool_max(m, parts=None):
+        def pool_max(pooled, y, m, parts=None):
             for n0, n1 in parts or token_parts(m):
                 nc.vector.tensor_reduce(
                     out=pooled[:, m, n0 // D : n1 // D],
@@ -163,46 +163,49 @@ def tile_picked_pool_lin_silu_sub_e_kernel(tc, xT, w, b, offs, out):
                     op=MAX,
                 )
 
+        s_copy, v_copy = nc.scalar.copy, nc.vector.tensor_copy
         out_view = out.rearrange("(t p) v -> p t v", p=P)
 
-        interleave(0, 0, EARLY * P, nc.scalar.copy)
-        gather(0, 0, 0, S)
-        quantize_w(0, 0, EARLY * P)
-        for a, j in PLANES[1:-1]:
-            gather(a, j, 0, S)
-        quantize_x(0, 0, S)
+        for m in range(EARLY):
+            interleave(s_copy, 0, m)
+        gather(0, 0)
+        for m in range(EARLY):
+            quantize_w(m, 0, 1)
+        for a, j, count in X_LOADS[1:-1]:
+            gather(a, j)
+        quantize_x(0)
         for m in range(EARLY):
             multiply(0, m)
         gather(1, 3, 0, HALF)
         gather(1, 3, HALF, S)
         for a, m in PIECES[:-2]:
-            interleave_late(a, m)
-        quantize_x(1, 0, HALF)
-        quantize_late(1, 0)
-        multiply(1, 0, [(0, HALF)])
-        quantize_x(1, HALF, S)
-        multiply(1, 0, [(HALF, S)])
-        quantize_late(1, 1)
-        multiply(1, 1)
-        quantize_late(0, 2)
+            interleave(s_copy, a, m)
+        quantize_w(2, 0, 1)
         multiply(0, 2)
-        interleave_late(0, LAST)
-        quantize_late(1, 2)
+        quantize_x(1, 0, HALF)
+        quantize_w(0, 1, 2)
+        multiply(1, 0, FIRST_HALF)
+        quantize_x(1, HALF, S)
+        multiply(1, 0, SECOND_HALF)
+        quantize_w(1, 1, 2)
+        multiply(1, 1)
+        interleave(v_copy, 0, LAST)
+        quantize_w(2, 1, 2)
         multiply(1, 2)
-        quantize_late(0, LAST)
+        quantize_w(LAST, 0, 1)
         multiply(0, LAST)
-        interleave_late(1, LAST)
-        y = keep.tile([P, M_TILES, S], F32, align_bytes=64, name="y", tag=f"raw_1_{(LAST - 1) * P}")
+        interleave(v_copy, 1, LAST)
+        y = keep.tile([P, M_TILES, S], F32, align_bytes=64, name="y", tag="raw_1_2")
         for m in range(LAST):
-            activate(m)
-        pooled = keep.tile([P, M_TILES, V], F32, align_bytes=64, name="pooled", tag=f"raw_1_{LAST * P}")
-        pool_max(0, [(0, HALF)])
-        quantize_late(1, LAST)
+            activate(y, m)
+        pooled = keep.tile([P, M_TILES, V], F32, align_bytes=64, name="pooled", tag="raw_1_3")
+        pool_max(pooled, y, 0, FIRST_HALF)
+        quantize_w(LAST, 1, 2)
         multiply(1, LAST)
-        activate(LAST)
-        pool_max(0, [(HALF, S)])
+        activate(y, LAST)
+        pool_max(pooled, y, 0, SECOND_HALF)
         for m in range(1, LAST):
-            pool_max(m)
+            pool_max(pooled, y, m)
         nc.sync.dma_start(out=out_view[:, 0:LAST, :], in_=pooled[:, 0:LAST, :])
-        pool_max(LAST)
+        pool_max(pooled, y, LAST)
         nc.sync.dma_start(out=out_view[:, LAST, :], in_=pooled[:, LAST, :])

@@ -25,11 +25,11 @@ HALF = S // 2
 HALVED = (0, 3)
 
 LAST = M_TILES - 1
+BANK = 512
+EARLY = 3
+PIECES = [(1, 0), (1, 1), (1, 2), (0, 3), (1, 3)]
 LAST_PLANE = (PASSES - 1, PACK - 1)
 FIRST_HALF, SECOND_HALF = [(0, HALF)], [(HALF, S)]
-EARLY = 2
-X_LOADS = [(0, 0, 1), (0, 1, 1), (0, 2, 1), (1, 0, 1), (1, 1, 1), (1, 2, 1), (0, 3, 1), (1, 3, 1)]
-PIECES = [(0, 2), (1, 0), (1, 1), (1, 2), (0, 3), (1, 3)]
 
 
 def token_parts(m):
@@ -66,16 +66,18 @@ def tile_picked_pool_lin_silu_sub_e_kernel(tc, xT, w, b, offs, out):
                 nc.sync.dma_start(out=table[:], in_=pass_rows(xT, a)[:, j, :])
                 planes[(a, j)] = table[:]
             else:
-                table = keep.tile([P, count, T], F32, align_bytes=64, name=f"planes_{a}_{j}")
+                table = keep.tile([P, count, T], F32, align_bytes=64, name=f"planes_{a}_{j}", tag=f"planes_{a}_{j}")
                 nc.sync.dma_start(out=table[:], in_=pass_rows(xT, a)[:, j : j + count, :])
                 for u in range(count):
                     planes[(a, j + u)] = table[:, u, :]
 
         offsets = lists.tile([P, S // 16], U16, name="offsets")
-        load_w(0, 0, EARLY)
+        load_x(0, 0, 2)
         nc.sync.dma_start(offsets[:], offs)
-        for a, j, count in X_LOADS:
-            load_x(a, j, count)
+        load_x(0, 2, 2)
+        load_w(0, 0, EARLY)
+        for j in range(PACK):
+            load_x(1, j)
         for a, m in PIECES:
             load_w(a, m)
 
@@ -85,11 +87,10 @@ def tile_picked_pool_lin_silu_sub_e_kernel(tc, xT, w, b, offs, out):
         nc.scalar.activation(warm_out[:], warm[:], SILU)
 
         ident = keep.tile([P, P], F32, name="ident")
-        bias = keep.tile([P, M_TILES], F32, name="bias")
+        bias = keep.tile([P, M_TILES], F32, align_bytes=64, name="bias", tag="planes_1_2")
         make_identity(nc, ident[:])
-        b_cols = psum.tile([P, P], F32, name="b_cols")
-        nc.tensor.transpose(b_cols[:], b_rows[:], ident[:])
-        nc.scalar.copy(bias[:], b_cols[:, 0:M_TILES])
+        b_cols = psum.tile([P, 4 * BANK], F32, offset=0, name="b_cols")
+        nc.tensor.transpose(b_cols[:, 0:P], b_rows[:], ident[:])
 
         x_grouped = [keep.tile([P, S, PACK], BF16, align_bytes=64, name=f"xg_{a}") for a in range(PASSES)]
         x_codes = [keep.tile([P, S], U32, align_bytes=64, name=f"xc_{a}") for a in range(PASSES)]
@@ -108,42 +109,46 @@ def tile_picked_pool_lin_silu_sub_e_kernel(tc, xT, w, b, offs, out):
                 in_=x_grouped[a][:, n0:n1, :].rearrange("p n j -> p (n j)"),
             )
 
-        def w_tile(m, dtype, columns, place, name):
-            if place is None:
-                return keep.tile([P, columns], dtype, align_bytes=64, name=name)
-            return late.tile([P, columns], dtype, align_bytes=64, offset=place, name=name)
+        w_grouped, w_codes, w_scales = {}, {}, {}
+        early_grouped = keep.tile([P, EARLY * P * PACK], BF16, align_bytes=64, name="wg_early")
+        early_codes = keep.tile([P, EARLY * P], U32, align_bytes=64, name="wc_early")
+        early_scales = keep.tile([P, EARLY * P], U8, align_bytes=64, name="ws_early")
+        for m in range(EARLY):
+            w_grouped[(0, m)] = early_grouped[:, m * P * PACK : (m + 1) * P * PACK]
+            w_codes[(0, m)] = early_codes[:, m * P : (m + 1) * P]
+            w_scales[(0, m)] = early_scales[:, m * P : (m + 1) * P]
+        for i, (a, m) in enumerate(PIECES):
+            if m == LAST:
+                grouped = late.tile([P, P * PACK], BF16, align_bytes=64, offset=4096 + 1024 * a, name=f"wg_{a}_{m}")
+            else:
+                grouped = keep.tile([P, P * PACK], BF16, align_bytes=64, name=f"wg_{a}_{m}")
+            codes = late.tile([P, P], U32, align_bytes=64, offset=512 * i, name=f"wc_{a}_{m}")
+            scales = keep.tile([P, P], U8, align_bytes=64, name=f"ws_{a}_{m}")
+            w_grouped[(a, m)], w_codes[(a, m)], w_scales[(a, m)] = grouped[:], codes[:], scales[:]
 
-        w_grouped = [w_tile(m, BF16, PASSES * P * PACK, None if m < LAST else 4096, f"wg_{m}") for m in range(M_TILES)]
-        w_codes = [w_tile(m, U32, PASSES * P, None if m < EARLY else 1024 * m, f"wc_{m}") for m in range(M_TILES)]
-        w_scales = [keep.tile([P, PASSES * P], U8, align_bytes=64, name=f"ws_{m}") for m in range(M_TILES)]
-
-        def interleave(copy, a, m, c0=0, c1=P):
+        def interleave(copy, a, m):
             for (pass_, first), raw in raws.items():
                 if pass_ == a and first <= m < first + raw.shape[2] // P:
                     base = (m - first) * P
                     copy(
-                        w_grouped[m][:, (a * P + c0) * PACK : (a * P + c1) * PACK].rearrange("p (c i j) -> p c j i", i=4, j=PACK),
-                        raw[:, :, base + c0 : base + c1].rearrange("p j (c i) -> p c j i", i=4),
+                        w_grouped[(a, m)].rearrange("p (c i j) -> p c j i", i=4, j=PACK),
+                        raw[:, :, base : base + P].rearrange("p j (c i) -> p c j i", i=4),
                     )
 
-        def quantize_w(m, a0=0, a1=PASSES):
-            nc.vector.quantize_mx(
-                out=w_codes[m][:, a0 * P : a1 * P].bitcast(FP8X4),
-                scales=w_scales[m][:, a0 * P : a1 * P],
-                in_=w_grouped[m][:, a0 * P * PACK : a1 * P * PACK],
-            )
+        def quantize_w(a, m):
+            nc.vector.quantize_mx(out=w_codes[(a, m)].bitcast(FP8X4), scales=w_scales[(a, m)], in_=w_grouped[(a, m)])
 
         acc = {}
         for m in range(M_TILES):
             for n0, n1 in token_parts(m):
-                acc[(m, n0)] = psum.tile([P, n1 - n0], F32, name=f"acc_{m}_{n0}")
+                acc[(m, n0)] = psum.tile([P, n1 - n0], F32, offset=4 * BANK * len(acc), name=f"acc_{m}_{n0}")
 
         def multiply(a, m, parts=None):
             for n0, n1 in parts or token_parts(m):
                 nc.tensor.matmul_mx(
                     out=acc[(m, n0)][:],
-                    lhsT=w_codes[m][:, a * P : (a + 1) * P].bitcast(FP8X4),
-                    lhsT_scale=w_scales[m][:, a * P : (a + 1) * P],
+                    lhsT=w_codes[(a, m)].bitcast(FP8X4),
+                    lhsT_scale=w_scales[(a, m)],
                     rhs=x_codes[a][:, n0:n1].bitcast(FP8X4),
                     rhs_scale=x_scales[a][:, n0:n1],
                     start=(a == 0),
@@ -151,14 +156,15 @@ def tile_picked_pool_lin_silu_sub_e_kernel(tc, xT, w, b, offs, out):
                 )
 
         def activate(y, m, parts=None):
-            for n0, n1 in parts or token_parts(m):
-                nc.scalar.activation(y[:, m, n0:n1], acc[(m, n0)][:], SILU, bias=bias[:, m : m + 1])
+            for n0, n1 in parts or FIRST_HALF + SECOND_HALF:
+                sums = acc[(m, n0)][:] if m in HALVED else acc[(m, 0)][:, n0:n1]
+                nc.scalar.activation(y[m][:, n0:n1], sums, SILU, bias=bias[:, m : m + 1])
 
         def pool_max(pooled, y, m, parts=None):
-            for n0, n1 in parts or token_parts(m):
+            for n0, n1 in parts or FIRST_HALF + SECOND_HALF:
                 nc.vector.tensor_reduce(
-                    out=pooled[:, m, n0 // D : n1 // D],
-                    in_=y[:, m, n0:n1].rearrange("p (v d) -> p v d", d=D),
+                    out=pooled[m][:, n0 // D : n1 // D],
+                    in_=y[m][:, n0:n1].rearrange("p (v d) -> p v d", d=D),
                     axis=AX,
                     op=MAX,
                 )
@@ -166,46 +172,53 @@ def tile_picked_pool_lin_silu_sub_e_kernel(tc, xT, w, b, offs, out):
         s_copy, v_copy = nc.scalar.copy, nc.vector.tensor_copy
         out_view = out.rearrange("(t p) v -> p t v", p=P)
 
+        for j in range(PACK):
+            gather(0, j)
+        quantize_x(0)
         for m in range(EARLY):
             interleave(s_copy, 0, m)
-        gather(0, 0)
-        for m in range(EARLY):
-            quantize_w(m, 0, 1)
-        for a, j, count in X_LOADS[1:-1]:
-            gather(a, j)
-        quantize_x(0)
+        gather(1, 0)
+        nc.vector.quantize_mx(
+            out=early_codes[:, 0 : 2 * P].bitcast(FP8X4),
+            scales=early_scales[:, 0 : 2 * P],
+            in_=early_grouped[:, 0 : 2 * P * PACK],
+        )
+        quantize_w(0, 2)
+        gather(1, 1)
+        gather(1, 2)
+        nc.scalar.copy(bias[:], b_cols[:, 0:M_TILES])
         for m in range(EARLY):
             multiply(0, m)
         gather(1, 3, 0, HALF)
         gather(1, 3, HALF, S)
-        for a, m in PIECES[:-2]:
+        for a, m in PIECES[:LAST]:
             interleave(s_copy, a, m)
-        quantize_w(2, 0, 1)
-        multiply(0, 2)
         quantize_x(1, 0, HALF)
-        quantize_w(0, 1, 2)
+        quantize_w(1, 0)
         multiply(1, 0, FIRST_HALF)
         quantize_x(1, HALF, S)
         multiply(1, 0, SECOND_HALF)
-        quantize_w(1, 1, 2)
+        quantize_w(1, 1)
         multiply(1, 1)
         interleave(v_copy, 0, LAST)
-        quantize_w(2, 1, 2)
+        quantize_w(1, 2)
         multiply(1, 2)
-        quantize_w(LAST, 0, 1)
+        quantize_w(0, LAST)
         multiply(0, LAST)
         interleave(v_copy, 1, LAST)
-        y = keep.tile([P, M_TILES, S], F32, align_bytes=64, name="y", tag="raw_1_2")
+        y_all = keep.tile([P, M_TILES, S], F32, align_bytes=64, name="y_all", tag="raw_1_2")
+        y = [y_all[:, m, :] for m in range(M_TILES)]
         for m in range(LAST):
             activate(y, m)
-        pooled = keep.tile([P, M_TILES, V], F32, align_bytes=64, name="pooled", tag="raw_1_3")
+        pooled_all = keep.tile([P, M_TILES, V], F32, align_bytes=64, name="pooled_all", tag="raw_1_3")
+        pooled = [pooled_all[:, m, :] for m in range(M_TILES)]
         pool_max(pooled, y, 0, FIRST_HALF)
-        quantize_w(LAST, 1, 2)
+        quantize_w(1, LAST)
         multiply(1, LAST)
         activate(y, LAST)
         pool_max(pooled, y, 0, SECOND_HALF)
         for m in range(1, LAST):
             pool_max(pooled, y, m)
-        nc.sync.dma_start(out=out_view[:, 0:LAST, :], in_=pooled[:, 0:LAST, :])
+        nc.sync.dma_start(out=out_view[:, 0:LAST, :], in_=pooled_all[:, 0:LAST, :])
         pool_max(pooled, y, LAST)
-        nc.sync.dma_start(out=out_view[:, LAST, :], in_=pooled[:, LAST, :])
+        nc.sync.dma_start(out=out_view[:, LAST, :], in_=pooled[LAST])

@@ -26,8 +26,8 @@ HALVED = (0, 3)
 
 LAST = M_TILES - 1
 BANK = 512
-EARLY = 3
-PIECES = [(1, 0), (1, 1), (1, 2), (0, 3), (1, 3)]
+EARLY = 4
+PIECES = [(1, 0), (1, 1), (1, 2), (1, 3)]
 LAST_PLANE = (PASSES - 1, PACK - 1)
 FIRST_HALF, SECOND_HALF = [(0, HALF)], [(HALF, S)]
 
@@ -89,7 +89,7 @@ def tile_picked_pool_lin_silu_sub_e_kernel(tc, xT, w, b, offs, out):
         ident = keep.tile([P, P], F32, name="ident")
         bias = keep.tile([P, M_TILES], F32, align_bytes=64, name="bias", tag="planes_1_2")
         make_identity(nc, ident[:])
-        b_cols = psum.tile([P, 4 * BANK], F32, offset=0, name="b_cols")
+        b_cols = psum.tile([P, 6 * BANK], F32, offset=0, name="b_cols")
         nc.tensor.transpose(b_cols[:, 0:P], b_rows[:], ident[:])
 
         x_grouped = [keep.tile([P, S, PACK], BF16, align_bytes=64, name=f"xg_{a}") for a in range(PASSES)]
@@ -178,12 +178,7 @@ def tile_picked_pool_lin_silu_sub_e_kernel(tc, xT, w, b, offs, out):
         for m in range(EARLY):
             interleave(s_copy, 0, m)
         gather(1, 0)
-        nc.vector.quantize_mx(
-            out=early_codes[:, 0 : 2 * P].bitcast(FP8X4),
-            scales=early_scales[:, 0 : 2 * P],
-            in_=early_grouped[:, 0 : 2 * P * PACK],
-        )
-        quantize_w(0, 2)
+        nc.vector.quantize_mx(out=early_codes[:].bitcast(FP8X4), scales=early_scales[:], in_=early_grouped[:])
         gather(1, 1)
         gather(1, 2)
         nc.scalar.copy(bias[:], b_cols[:, 0:M_TILES])
@@ -200,12 +195,9 @@ def tile_picked_pool_lin_silu_sub_e_kernel(tc, xT, w, b, offs, out):
         multiply(1, 0, SECOND_HALF)
         quantize_w(1, 1)
         multiply(1, 1)
-        interleave(v_copy, 0, LAST)
+        interleave(v_copy, 1, LAST)
         quantize_w(1, 2)
         multiply(1, 2)
-        quantize_w(0, LAST)
-        multiply(0, LAST)
-        interleave(v_copy, 1, LAST)
         y_all = keep.tile([P, M_TILES, S], F32, align_bytes=64, name="y_all", tag="raw_1_2")
         y = [y_all[:, m, :] for m in range(M_TILES)]
         for m in range(LAST):

@@ -13,6 +13,7 @@ U16 = mybir.dt.uint16
 U8 = mybir.dt.uint8
 FP8X4 = mybir.dt.float8_e4m3fn_x4
 SILU = mybir.ActivationFunctionType.Silu
+COPY = mybir.ActivationFunctionType.Copy
 AX = mybir.AxisListType.X
 MAX = mybir.AluOpType.max
 
@@ -22,7 +23,7 @@ K_PASS = P * PACK
 PASSES = K // K_PASS
 M_TILES = N // P
 HALF = S // 2
-HALVED = (0, 3)
+HALVED = (0, 1, 2, 3)
 
 LAST = M_TILES - 1
 BANK = 512
@@ -30,6 +31,7 @@ EARLY = 4
 PIECES = [(1, 0), (1, 1), (1, 2), (1, 3)]
 LAST_PLANE = (PASSES - 1, PACK - 1)
 FIRST_HALF, SECOND_HALF = [(0, HALF)], [(HALF, S)]
+SPLITS = (384, 256)
 
 
 def token_parts(m):
@@ -72,12 +74,12 @@ def tile_picked_pool_lin_silu_sub_e_kernel(tc, xT, w, b, offs, out):
                     planes[(a, j + u)] = table[:, u, :]
 
         offsets = lists.tile([P, S // 16], U16, name="offsets")
-        load_x(0, 0, 2)
+        load_x(0, 0, 4)
         nc.sync.dma_start(offsets[:], offs)
-        load_x(0, 2, 2)
         load_w(0, 0, EARLY)
-        for j in range(PACK):
-            load_x(1, j)
+        load_x(1, 0, 2)
+        load_x(1, 2)
+        load_x(1, 3)
         for a, m in PIECES:
             load_w(a, m)
 
@@ -89,12 +91,20 @@ def tile_picked_pool_lin_silu_sub_e_kernel(tc, xT, w, b, offs, out):
         ident = keep.tile([P, P], F32, name="ident")
         bias = keep.tile([P, M_TILES], F32, align_bytes=64, name="bias", tag="planes_1_2")
         make_identity(nc, ident[:])
-        b_cols = psum.tile([P, 6 * BANK], F32, offset=0, name="b_cols")
+        b_cols = psum.tile([P, 8 * BANK], F32, offset=0, name="b_cols")
         nc.tensor.transpose(b_cols[:, 0:P], b_rows[:], ident[:])
 
         x_grouped = [keep.tile([P, S, PACK], BF16, align_bytes=64, name=f"xg_{a}") for a in range(PASSES)]
         x_codes = [keep.tile([P, S], U32, align_bytes=64, name=f"xc_{a}") for a in range(PASSES)]
-        x_scales = [keep.tile([P, S], U8, align_bytes=64, name=f"xs_{a}") for a in range(PASSES)]
+        early_x_scales = keep.tile([P, S], U8, align_bytes=64, name="xs_0")
+        late_x_scales = [
+            keep.tile([P, HALF], U8, align_bytes=64, name="xs_1_first"),
+            keep.tile([P, HALF], U8, align_bytes=64, name="xs_1_second", tag="raw_1_0"),
+        ]
+
+        def x_scales(a, n0, n1):
+            return early_x_scales[:, n0:n1] if a == 0 else late_x_scales[n0 // HALF][:]
+
 
         def gather(a, j, n0=0, n1=S):
             nc.vector.tensor_copy(
@@ -102,10 +112,17 @@ def tile_picked_pool_lin_silu_sub_e_kernel(tc, xT, w, b, offs, out):
                 in_=planes[(a, j)].indirect(offsets[:, n0 // 16 : n1 // 16]),
             )
 
+        def scalar_share(a, count):
+            n0 = SPLITS[a]
+            dense = keep.tile([P, count, S - n0], F32, align_bytes=64, name=f"dense_{a}")
+            for j in range(count):
+                nc.scalar.activation(dense[:, j, :], planes[(a, j)].indirect(offsets[:, n0 // 16 : S // 16]), COPY)
+            nc.scalar.copy(x_grouped[a][:, n0:S, 0:count], dense[:].rearrange("p j n -> p n j"))
+
         def quantize_x(a, n0=0, n1=S):
             nc.vector.quantize_mx(
                 out=x_codes[a][:, n0:n1].bitcast(FP8X4),
-                scales=x_scales[a][:, n0:n1],
+                scales=x_scales(a, n0, n1),
                 in_=x_grouped[a][:, n0:n1, :].rearrange("p n j -> p (n j)"),
             )
 
@@ -144,15 +161,15 @@ def tile_picked_pool_lin_silu_sub_e_kernel(tc, xT, w, b, offs, out):
                 acc[(m, n0)] = psum.tile([P, n1 - n0], F32, offset=4 * BANK * len(acc), name=f"acc_{m}_{n0}")
 
         def multiply(a, m, parts=None):
-            for n0, n1 in parts or token_parts(m):
+            for n0, n1 in parts or (token_parts(m) if a == 0 else FIRST_HALF + SECOND_HALF):
                 nc.tensor.matmul_mx(
-                    out=acc[(m, n0)][:],
+                    out=acc[(m, n0)][:] if m in HALVED else acc[(m, 0)][:, n0:n1],
                     lhsT=w_codes[(a, m)].bitcast(FP8X4),
                     lhsT_scale=w_scales[(a, m)],
                     rhs=x_codes[a][:, n0:n1].bitcast(FP8X4),
-                    rhs_scale=x_scales[a][:, n0:n1],
+                    rhs_scale=x_scales(a, n0, n1),
                     start=(a == 0),
-                    stop=(a == PASSES - 1),
+                    stop=(a == PASSES - 1 and (m in HALVED or n1 == S)),
                 )
 
         def activate(y, m, parts=None):
@@ -173,13 +190,15 @@ def tile_picked_pool_lin_silu_sub_e_kernel(tc, xT, w, b, offs, out):
         out_view = out.rearrange("(t p) v -> p t v", p=P)
 
         for j in range(PACK):
-            gather(0, j)
+            gather(0, j, 0, SPLITS[0])
+        scalar_share(0, PACK)
         quantize_x(0)
         for m in range(EARLY):
             interleave(s_copy, 0, m)
-        gather(1, 0)
+        gather(1, 0, 0, SPLITS[1])
+        gather(1, 1, 0, SPLITS[1])
+        scalar_share(1, 2)
         nc.vector.quantize_mx(out=early_codes[:].bitcast(FP8X4), scales=early_scales[:], in_=early_grouped[:])
-        gather(1, 1)
         gather(1, 2)
         nc.scalar.copy(bias[:], b_cols[:, 0:M_TILES])
         for m in range(EARLY):

@@ -16,6 +16,8 @@ SILU = mybir.ActivationFunctionType.Silu
 COPY = mybir.ActivationFunctionType.Copy
 AX = mybir.AxisListType.X
 MAX = mybir.AluOpType.max
+MULT = mybir.AluOpType.mult
+ADD = mybir.AluOpType.add
 
 P = 128
 PACK = 4
@@ -31,6 +33,7 @@ EARLY = 4
 PIECES = [(1, 0), (1, 1), (1, 2), (1, 3)]
 LAST_PLANE = (PASSES - 1, PACK - 1)
 FIRST_HALF, SECOND_HALF = [(0, HALF)], [(HALF, S)]
+TAIL_SPLIT = 384
 SPLITS = (384, 256)
 
 
@@ -71,7 +74,7 @@ def tile_picked_pool_lin_silu_sub_e_kernel(tc, xT, w, b, offs, out):
                 table = keep.tile([P, count, T], F32, align_bytes=64, name=f"planes_{a}_{j}", tag=f"planes_{a}_{j}")
                 nc.sync.dma_start(out=table[:], in_=pass_rows(xT, a)[:, j : j + count, :])
                 for u in range(count):
-                    planes[(a, j + u)] = table[:, u, :]
+                    planes[(a, j + u)] = table[:, u, :] if count > 1 else table[:].rearrange("p u t -> p (u t)")
 
         offsets = lists.tile([P, S // 16], U16, name="offsets")
         load_x(0, 0, 4)
@@ -174,7 +177,8 @@ def tile_picked_pool_lin_silu_sub_e_kernel(tc, xT, w, b, offs, out):
 
         def activate(y, m, parts=None):
             for n0, n1 in parts or FIRST_HALF + SECOND_HALF:
-                sums = acc[(m, n0)][:] if m in HALVED else acc[(m, 0)][:, n0:n1]
+                h0 = n0 // HALF * HALF
+                sums = acc[(m, h0)][:, n0 - h0 : n1 - h0]
                 nc.scalar.activation(y[m][:, n0:n1], sums, SILU, bias=bias[:, m : m + 1])
 
         def pool_max(pooled, y, m, parts=None):
@@ -199,13 +203,25 @@ def tile_picked_pool_lin_silu_sub_e_kernel(tc, xT, w, b, offs, out):
         gather(1, 1, 0, SPLITS[1])
         scalar_share(1, 2)
         nc.vector.quantize_mx(out=early_codes[:].bitcast(FP8X4), scales=early_scales[:], in_=early_grouped[:])
-        gather(1, 2)
+        gather(1, 2, 0, TAIL_SPLIT)
+        tail_dense = keep.tile([P, 2, S - TAIL_SPLIT], BF16, align_bytes=64, name="tail_dense")
+        tail_list = offsets[:, TAIL_SPLIT // 16 : S // 16]
+        nc.scalar.activation(tail_dense[:, 0, :], planes[(1, 2)].indirect(tail_list), COPY)
         nc.scalar.copy(bias[:], b_cols[:, 0:M_TILES])
         for m in range(EARLY):
             multiply(0, m)
-        gather(1, 3, 0, HALF)
-        gather(1, 3, HALF, S)
-        for a, m in PIECES[:LAST]:
+        gather(1, 3, 0, TAIL_SPLIT)
+        nc.scalar.activation(tail_dense[:, 1, :], planes[(1, 3)].indirect(tail_list), COPY)
+        nc.scalar.copy(x_grouped[1][:, TAIL_SPLIT:S, 2:PACK], tail_dense[:].rearrange("p e n -> p n e"))
+        nc.gpsimd.tensor_scalar(
+            w_grouped[(1, 0)].rearrange("p (c j) -> p c j", j=PACK),
+            raws[(1, 0)][:].rearrange("p j c -> p c j"),
+            1.0,
+            0.0,
+            op0=MULT,
+            op1=ADD,
+        )
+        for a, m in PIECES[1:LAST]:
             interleave(s_copy, a, m)
         quantize_x(1, 0, HALF)
         quantize_w(1, 0)
@@ -226,10 +242,11 @@ def tile_picked_pool_lin_silu_sub_e_kernel(tc, xT, w, b, offs, out):
         pool_max(pooled, y, 0, FIRST_HALF)
         quantize_w(1, LAST)
         multiply(1, LAST)
-        activate(y, LAST)
+        ending = FIRST_HALF + [(HALF, HALF + P), (HALF + P, S)]
+        activate(y, LAST, ending)
         pool_max(pooled, y, 0, SECOND_HALF)
         for m in range(1, LAST):
             pool_max(pooled, y, m)
         nc.sync.dma_start(out=out_view[:, 0:LAST, :], in_=pooled_all[:, 0:LAST, :])
-        pool_max(pooled, y, LAST)
+        pool_max(pooled, y, LAST, ending)
         nc.sync.dma_start(out=out_view[:, LAST, :], in_=pooled[LAST])

@@ -24,21 +24,24 @@ PACK = 4
 K_PASS = P * PACK
 PASSES = K // K_PASS
 M_TILES = N // P
-HALF = S // 2
-HALVED = (0, 1, 2, 3)
-
 LAST = M_TILES - 1
+STRIPE = 16
 BANK = 512
-EARLY = 4
-PIECES = [(1, 0), (1, 1), (1, 2), (1, 3)]
-LAST_PLANE = (PASSES - 1, PACK - 1)
-FIRST_HALF, SECOND_HALF = [(0, HALF)], [(HALF, S)]
+BANK_BYTES = 4 * BANK
+RUN = 4
+
+HALF = S // 2
+QUARTER = S // 4
+FIRST_HALF, SECOND_HALF = (0, HALF), (HALF, S)
+HALVES = [FIRST_HALF, SECOND_HALF]
+ENDING = [FIRST_HALF, (HALF, HALF + QUARTER), (HALF + QUARTER, S)]
+
+PASS_0_SPLIT = 384
+PAIR_SPLIT = 256
 TAIL_SPLIT = 384
-SPLITS = (384, 256)
 
-
-def token_parts(m):
-    return FIRST_HALF + SECOND_HALF if m in HALVED else [(0, S)]
+CODE_BYTES = 4 * P
+LAST_GROUPED_OFFSET = 5120
 
 
 def tile_picked_pool_lin_silu_sub_e_kernel(tc, xT, w, b, offs, out):
@@ -56,35 +59,34 @@ def tile_picked_pool_lin_silu_sub_e_kernel(tc, xT, w, b, offs, out):
         def pass_rows(tensor, a):
             return tensor[a * K_PASS : (a + 1) * K_PASS, :].rearrange("(p j) n -> p j n", j=PACK)
 
-        raws = {}
+        planes = {}
+        w_raw = {}
 
-        def load_w(a, m, tiles=1):
+        def load_planes(a, j, count):
+            table = keep.tile([P, count, T], F32, align_bytes=64, name=f"planes_{a}_{j}")
+            nc.sync.dma_start(out=table[:], in_=pass_rows(xT, a)[:, j : j + count, :])
+            for u in range(count):
+                planes[(a, j + u)] = table[:, u, :]
+
+        def load_w(a, m, tiles):
             raw = keep.tile([P, PACK, tiles * P], F32, align_bytes=64, name=f"raw_{a}_{m}", tag=f"raw_{a}_{m}")
             nc.sync.dma_start(out=raw[:], in_=pass_rows(w, a)[:, :, m * P : (m + tiles) * P])
-            raws[(a, m)] = raw
+            for u in range(tiles):
+                w_raw[(a, m + u)] = (raw, u * P)
 
-        planes = {}
-
-        def load_x(a, j, count=1):
-            if (a, j) == LAST_PLANE:
-                table = late.tile([P, T], F32, align_bytes=64, offset=0, name="last_plane")
-                nc.sync.dma_start(out=table[:], in_=pass_rows(xT, a)[:, j, :])
-                planes[(a, j)] = table[:]
-            else:
-                table = keep.tile([P, count, T], F32, align_bytes=64, name=f"planes_{a}_{j}", tag=f"planes_{a}_{j}")
-                nc.sync.dma_start(out=table[:], in_=pass_rows(xT, a)[:, j : j + count, :])
-                for u in range(count):
-                    planes[(a, j + u)] = table[:, u, :] if count > 1 else table[:].rearrange("p u t -> p (u t)")
-
-        offsets = lists.tile([P, S // 16], U16, name="offsets")
-        load_x(0, 0, 4)
+        offsets = lists.tile([P, S // STRIPE], U16, name="offsets")
+        load_planes(0, 0, PACK)
         nc.sync.dma_start(offsets[:], offs)
-        load_w(0, 0, EARLY)
-        load_x(1, 0, 2)
-        load_x(1, 2)
-        load_x(1, 3)
-        for a, m in PIECES:
-            load_w(a, m)
+        load_w(0, 0, M_TILES)
+        load_planes(1, 0, 2)
+        third_plane = keep.tile([P, 1, T], F32, align_bytes=64, name="third_plane", tag="third_plane")
+        nc.sync.dma_start(out=third_plane[:], in_=pass_rows(xT, 1)[:, 2:3, :])
+        planes[(1, 2)] = third_plane[:].rearrange("p u t -> p (u t)")
+        last_plane = late.tile([P, T], F32, align_bytes=64, offset=0, name="last_plane")
+        nc.sync.dma_start(out=last_plane[:], in_=pass_rows(xT, 1)[:, 3, :])
+        planes[(1, 3)] = last_plane[:]
+        for m in range(M_TILES):
+            load_w(1, m, 1)
 
         warm = keep.tile([P, 1], F32, name="warm")
         warm_out = keep.tile([P, 1], F32, name="warm_out")
@@ -92,37 +94,35 @@ def tile_picked_pool_lin_silu_sub_e_kernel(tc, xT, w, b, offs, out):
         nc.scalar.activation(warm_out[:], warm[:], SILU)
 
         ident = keep.tile([P, P], F32, name="ident")
-        bias = keep.tile([P, M_TILES], F32, align_bytes=64, name="bias", tag="planes_1_2")
+        bias = keep.tile([P, M_TILES], F32, align_bytes=64, name="bias", tag="third_plane")
         make_identity(nc, ident[:])
-        b_cols = psum.tile([P, 8 * BANK], F32, offset=0, name="b_cols")
+        b_cols = psum.tile([P, len(HALVES) * M_TILES * BANK], F32, offset=0, name="b_cols")
         nc.tensor.transpose(b_cols[:, 0:P], b_rows[:], ident[:])
 
         x_grouped = [keep.tile([P, S, PACK], BF16, align_bytes=64, name=f"xg_{a}") for a in range(PASSES)]
         x_codes = [keep.tile([P, S], U32, align_bytes=64, name=f"xc_{a}") for a in range(PASSES)]
-        early_x_scales = keep.tile([P, S], U8, align_bytes=64, name="xs_0")
-        late_x_scales = [
+        pass_0_x_scales = keep.tile([P, S], U8, align_bytes=64, name="xs_0")
+        pass_1_x_scales = [
             keep.tile([P, HALF], U8, align_bytes=64, name="xs_1_first"),
             keep.tile([P, HALF], U8, align_bytes=64, name="xs_1_second", tag="raw_1_0"),
         ]
 
         def x_scales(a, n0, n1):
-            return early_x_scales[:, n0:n1] if a == 0 else late_x_scales[n0 // HALF][:]
+            return pass_0_x_scales[:, n0:n1] if a == 0 else pass_1_x_scales[n0 // HALF][:]
 
+        def picked(a, j, n0, n1):
+            return planes[(a, j)].indirect(offsets[:, n0 // STRIPE : n1 // STRIPE])
 
-        def gather(a, j, n0=0, n1=S):
-            nc.vector.tensor_copy(
-                out=x_grouped[a][:, n0:n1, j],
-                in_=planes[(a, j)].indirect(offsets[:, n0 // 16 : n1 // 16]),
-            )
+        def vector_gather(a, j, split):
+            nc.vector.tensor_copy(out=x_grouped[a][:, 0:split, j], in_=picked(a, j, 0, split))
 
-        def scalar_share(a, count):
-            n0 = SPLITS[a]
-            dense = keep.tile([P, count, S - n0], F32, align_bytes=64, name=f"dense_{a}")
+        def scalar_share(a, count, split):
+            dense = keep.tile([P, count, S - split], F32, align_bytes=64, name=f"dense_{a}")
             for j in range(count):
-                nc.scalar.activation(dense[:, j, :], planes[(a, j)].indirect(offsets[:, n0 // 16 : S // 16]), COPY)
-            nc.scalar.copy(x_grouped[a][:, n0:S, 0:count], dense[:].rearrange("p j n -> p n j"))
+                nc.scalar.activation(dense[:, j, :], picked(a, j, split, S), COPY)
+            nc.scalar.copy(x_grouped[a][:, split:S, 0:count], dense[:].rearrange("p j n -> p n j"))
 
-        def quantize_x(a, n0=0, n1=S):
+        def quantize_x(a, n0, n1):
             nc.vector.quantize_mx(
                 out=x_codes[a][:, n0:n1].bitcast(FP8X4),
                 scales=x_scales(a, n0, n1),
@@ -130,123 +130,118 @@ def tile_picked_pool_lin_silu_sub_e_kernel(tc, xT, w, b, offs, out):
             )
 
         w_grouped, w_codes, w_scales = {}, {}, {}
-        early_grouped = keep.tile([P, EARLY * P * PACK], BF16, align_bytes=64, name="wg_early")
-        early_codes = keep.tile([P, EARLY * P], U32, align_bytes=64, name="wc_early")
-        early_scales = keep.tile([P, EARLY * P], U8, align_bytes=64, name="ws_early")
-        for m in range(EARLY):
-            w_grouped[(0, m)] = early_grouped[:, m * P * PACK : (m + 1) * P * PACK]
-            w_codes[(0, m)] = early_codes[:, m * P : (m + 1) * P]
-            w_scales[(0, m)] = early_scales[:, m * P : (m + 1) * P]
-        for i, (a, m) in enumerate(PIECES):
+        pass_0_grouped = keep.tile([P, N * PACK], BF16, align_bytes=64, name="wg_0")
+        pass_0_codes = keep.tile([P, N], U32, align_bytes=64, name="wc_0")
+        pass_0_scales = keep.tile([P, N], U8, align_bytes=64, name="ws_0")
+        for m in range(M_TILES):
+            w_grouped[(0, m)] = pass_0_grouped[:, m * P * PACK : (m + 1) * P * PACK]
+            w_codes[(0, m)] = pass_0_codes[:, m * P : (m + 1) * P]
+            w_scales[(0, m)] = pass_0_scales[:, m * P : (m + 1) * P]
+        for m in range(M_TILES):
             if m == LAST:
-                grouped = late.tile([P, P * PACK], BF16, align_bytes=64, offset=4096 + 1024 * a, name=f"wg_{a}_{m}")
+                grouped = late.tile([P, P * PACK], BF16, align_bytes=64, offset=LAST_GROUPED_OFFSET, name=f"wg_1_{m}")
             else:
-                grouped = keep.tile([P, P * PACK], BF16, align_bytes=64, name=f"wg_{a}_{m}")
-            codes = late.tile([P, P], U32, align_bytes=64, offset=512 * i, name=f"wc_{a}_{m}")
-            scales = keep.tile([P, P], U8, align_bytes=64, name=f"ws_{a}_{m}")
-            w_grouped[(a, m)], w_codes[(a, m)], w_scales[(a, m)] = grouped[:], codes[:], scales[:]
+                grouped = keep.tile([P, P * PACK], BF16, align_bytes=64, name=f"wg_1_{m}", tag=f"wg_1_{m}")
+            codes = late.tile([P, P], U32, align_bytes=64, offset=CODE_BYTES * m, name=f"wc_1_{m}")
+            scales = keep.tile([P, P], U8, align_bytes=64, name=f"ws_1_{m}")
+            w_grouped[(1, m)], w_codes[(1, m)], w_scales[(1, m)] = grouped[:], codes[:], scales[:]
 
         def interleave(copy, a, m):
-            for (pass_, first), raw in raws.items():
-                if pass_ == a and first <= m < first + raw.shape[2] // P:
-                    base = (m - first) * P
-                    copy(
-                        w_grouped[(a, m)].rearrange("p (c i j) -> p c j i", i=4, j=PACK),
-                        raw[:, :, base : base + P].rearrange("p j (c i) -> p c j i", i=4),
-                    )
+            raw, first = w_raw[(a, m)]
+            copy(
+                w_grouped[(a, m)].rearrange("p (c i j) -> p c j i", i=RUN, j=PACK),
+                raw[:, :, first : first + P].rearrange("p j (c i) -> p c j i", i=RUN),
+            )
 
-        def quantize_w(a, m):
-            nc.vector.quantize_mx(out=w_codes[(a, m)].bitcast(FP8X4), scales=w_scales[(a, m)], in_=w_grouped[(a, m)])
+        def quantize_w(m):
+            nc.vector.quantize_mx(out=w_codes[(1, m)].bitcast(FP8X4), scales=w_scales[(1, m)], in_=w_grouped[(1, m)])
 
-        acc = {}
+        sums = {}
         for m in range(M_TILES):
-            for n0, n1 in token_parts(m):
-                acc[(m, n0)] = psum.tile([P, n1 - n0], F32, offset=4 * BANK * len(acc), name=f"acc_{m}_{n0}")
+            for n0, n1 in HALVES:
+                sums[(m, n0)] = psum.tile([P, HALF], F32, offset=BANK_BYTES * len(sums), name=f"sums_{m}_{n0}")
 
-        def multiply(a, m, parts=None):
-            for n0, n1 in parts or (token_parts(m) if a == 0 else FIRST_HALF + SECOND_HALF):
+        def multiply(a, m, parts):
+            for n0, n1 in parts:
                 nc.tensor.matmul_mx(
-                    out=acc[(m, n0)][:] if m in HALVED else acc[(m, 0)][:, n0:n1],
+                    out=sums[(m, n0)][:],
                     lhsT=w_codes[(a, m)].bitcast(FP8X4),
                     lhsT_scale=w_scales[(a, m)],
                     rhs=x_codes[a][:, n0:n1].bitcast(FP8X4),
                     rhs_scale=x_scales(a, n0, n1),
                     start=(a == 0),
-                    stop=(a == PASSES - 1 and (m in HALVED or n1 == S)),
+                    stop=(a == PASSES - 1),
                 )
 
-        def activate(y, m, parts=None):
-            for n0, n1 in parts or FIRST_HALF + SECOND_HALF:
+        def activate(y, m, parts):
+            for n0, n1 in parts:
                 h0 = n0 // HALF * HALF
-                sums = acc[(m, h0)][:, n0 - h0 : n1 - h0]
-                nc.scalar.activation(y[m][:, n0:n1], sums, SILU, bias=bias[:, m : m + 1])
+                nc.scalar.activation(
+                    y[:, m, :][:, n0:n1], sums[(m, h0)][:, n0 - h0 : n1 - h0], SILU, bias=bias[:, m : m + 1]
+                )
 
-        def pool_max(pooled, y, m, parts=None):
-            for n0, n1 in parts or FIRST_HALF + SECOND_HALF:
+        def pool_max(pooled, y, m, parts):
+            for n0, n1 in parts:
                 nc.vector.tensor_reduce(
-                    out=pooled[m][:, n0 // D : n1 // D],
-                    in_=y[m][:, n0:n1].rearrange("p (v d) -> p v d", d=D),
+                    out=pooled[:, m, :][:, n0 // D : n1 // D],
+                    in_=y[:, m, :][:, n0:n1].rearrange("p (v d) -> p v d", d=D),
                     axis=AX,
                     op=MAX,
                 )
 
-        s_copy, v_copy = nc.scalar.copy, nc.vector.tensor_copy
         out_view = out.rearrange("(t p) v -> p t v", p=P)
 
         for j in range(PACK):
-            gather(0, j, 0, SPLITS[0])
-        scalar_share(0, PACK)
-        quantize_x(0)
-        for m in range(EARLY):
-            interleave(s_copy, 0, m)
-        gather(1, 0, 0, SPLITS[1])
-        gather(1, 1, 0, SPLITS[1])
-        scalar_share(1, 2)
-        nc.vector.quantize_mx(out=early_codes[:].bitcast(FP8X4), scales=early_scales[:], in_=early_grouped[:])
-        gather(1, 2, 0, TAIL_SPLIT)
+            vector_gather(0, j, PASS_0_SPLIT)
+        scalar_share(0, PACK, PASS_0_SPLIT)
+        quantize_x(0, 0, S)
+        for m in range(M_TILES):
+            interleave(nc.scalar.copy, 0, m)
+        for j in range(2):
+            vector_gather(1, j, PAIR_SPLIT)
+        scalar_share(1, 2, PAIR_SPLIT)
+        nc.vector.quantize_mx(out=pass_0_codes[:].bitcast(FP8X4), scales=pass_0_scales[:], in_=pass_0_grouped[:])
+        vector_gather(1, 2, TAIL_SPLIT)
         tail_dense = keep.tile([P, 2, S - TAIL_SPLIT], BF16, align_bytes=64, name="tail_dense")
-        tail_list = offsets[:, TAIL_SPLIT // 16 : S // 16]
-        nc.scalar.activation(tail_dense[:, 0, :], planes[(1, 2)].indirect(tail_list), COPY)
+        nc.scalar.activation(tail_dense[:, 0, :], picked(1, 2, TAIL_SPLIT, S), COPY)
         nc.scalar.copy(bias[:], b_cols[:, 0:M_TILES])
-        for m in range(EARLY):
-            multiply(0, m)
-        gather(1, 3, 0, TAIL_SPLIT)
-        nc.scalar.activation(tail_dense[:, 1, :], planes[(1, 3)].indirect(tail_list), COPY)
+        for m in range(M_TILES):
+            multiply(0, m, HALVES)
+
+        vector_gather(1, 3, TAIL_SPLIT)
+        nc.scalar.activation(tail_dense[:, 1, :], picked(1, 3, TAIL_SPLIT, S), COPY)
         nc.scalar.copy(x_grouped[1][:, TAIL_SPLIT:S, 2:PACK], tail_dense[:].rearrange("p e n -> p n e"))
         nc.gpsimd.tensor_scalar(
             w_grouped[(1, 0)].rearrange("p (c j) -> p c j", j=PACK),
-            raws[(1, 0)][:].rearrange("p j c -> p c j"),
+            w_raw[(1, 0)][0][:].rearrange("p j c -> p c j"),
             1.0,
             0.0,
             op0=MULT,
             op1=ADD,
         )
-        for a, m in PIECES[1:LAST]:
-            interleave(s_copy, a, m)
-        quantize_x(1, 0, HALF)
-        quantize_w(1, 0)
-        multiply(1, 0, FIRST_HALF)
-        quantize_x(1, HALF, S)
-        multiply(1, 0, SECOND_HALF)
-        quantize_w(1, 1)
-        multiply(1, 1)
-        interleave(v_copy, 1, LAST)
-        quantize_w(1, 2)
-        multiply(1, 2)
-        y_all = keep.tile([P, M_TILES, S], F32, align_bytes=64, name="y_all", tag="raw_1_2")
-        y = [y_all[:, m, :] for m in range(M_TILES)]
-        for m in range(LAST):
-            activate(y, m)
-        pooled_all = keep.tile([P, M_TILES, V], F32, align_bytes=64, name="pooled_all", tag="raw_1_3")
-        pooled = [pooled_all[:, m, :] for m in range(M_TILES)]
-        pool_max(pooled, y, 0, FIRST_HALF)
-        quantize_w(1, LAST)
-        multiply(1, LAST)
-        ending = FIRST_HALF + [(HALF, HALF + P), (HALF + P, S)]
-        activate(y, LAST, ending)
-        pool_max(pooled, y, 0, SECOND_HALF)
         for m in range(1, LAST):
-            pool_max(pooled, y, m)
-        nc.sync.dma_start(out=out_view[:, 0:LAST, :], in_=pooled_all[:, 0:LAST, :])
-        pool_max(pooled, y, LAST, ending)
-        nc.sync.dma_start(out=out_view[:, LAST, :], in_=pooled[LAST])
+            interleave(nc.scalar.copy, 1, m)
+        quantize_x(1, *FIRST_HALF)
+        quantize_w(0)
+        multiply(1, 0, [FIRST_HALF])
+        quantize_x(1, *SECOND_HALF)
+        multiply(1, 0, [SECOND_HALF])
+        quantize_w(1)
+        multiply(1, 1, HALVES)
+        interleave(nc.vector.tensor_copy, 1, LAST)
+        quantize_w(2)
+        multiply(1, 2, HALVES)
+        y = keep.tile([P, M_TILES, S], F32, align_bytes=64, name="y", tag="wg_1_1")
+        for m in range(LAST):
+            activate(y, m, HALVES)
+        pooled = keep.tile([P, M_TILES, V], F32, align_bytes=64, name="pooled", tag="raw_1_3")
+        pool_max(pooled, y, 0, [FIRST_HALF])
+        quantize_w(LAST)
+        multiply(1, LAST, HALVES)
+        activate(y, LAST, ENDING)
+        pool_max(pooled, y, 0, [SECOND_HALF])
+        for m in range(1, LAST):
+            pool_max(pooled, y, m, HALVES)
+        nc.sync.dma_start(out=out_view[:, 0:LAST, :], in_=pooled[:, 0:LAST, :])
+        pool_max(pooled, y, LAST, ENDING)
+        nc.sync.dma_start(out=out_view[:, LAST, :], in_=pooled[:, LAST, :])

@@ -40,6 +40,8 @@ PASS_0_SPLIT = 384
 PAIR_SPLIT = 256
 TAIL_SPLIT = 384
 
+LAST_SPLIT = 96
+
 CODE_BYTES = 4 * P
 LAST_GROUPED_OFFSET = 5120
 
@@ -146,11 +148,11 @@ def tile_picked_pool_lin_silu_sub_e_kernel(tc, xT, w, b, offs, out):
             scales = keep.tile([P, P], U8, align_bytes=64, name=f"ws_1_{m}")
             w_grouped[(1, m)], w_codes[(1, m)], w_scales[(1, m)] = grouped[:], codes[:], scales[:]
 
-        def interleave(copy, a, m):
+        def interleave(copy, a, m, c0=0, c1=P):
             raw, first = w_raw[(a, m)]
             copy(
-                w_grouped[(a, m)].rearrange("p (c i j) -> p c j i", i=RUN, j=PACK),
-                raw[:, :, first : first + P].rearrange("p j (c i) -> p c j i", i=RUN),
+                w_grouped[(a, m)][:, c0 * PACK : c1 * PACK].rearrange("p (c i j) -> p c j i", i=RUN, j=PACK),
+                raw[:, :, first + c0 : first + c1].rearrange("p j (c i) -> p c j i", i=RUN),
             )
 
         def quantize_w(m):
@@ -228,13 +230,16 @@ def tile_picked_pool_lin_silu_sub_e_kernel(tc, xT, w, b, offs, out):
         multiply(1, 0, [SECOND_HALF])
         quantize_w(1)
         multiply(1, 1, HALVES)
-        interleave(nc.vector.tensor_copy, 1, LAST)
+        interleave(nc.vector.tensor_copy, 1, LAST, 0, LAST_SPLIT)
         quantize_w(2)
         multiply(1, 2, HALVES)
         y = keep.tile([P, M_TILES, S], F32, align_bytes=64, name="y", tag="wg_1_1")
-        for m in range(LAST):
+        activate(y, 0, [FIRST_HALF])
+        interleave(nc.scalar.copy, 1, LAST, LAST_SPLIT, P)
+        activate(y, 0, [SECOND_HALF])
+        for m in range(1, LAST):
             activate(y, m, HALVES)
-        pooled = keep.tile([P, M_TILES, V], F32, align_bytes=64, name="pooled", tag="raw_1_3")
+        pooled = keep.tile([P, M_TILES, V], F32, align_bytes=64, name="pooled")
         pool_max(pooled, y, 0, [FIRST_HALF])
         quantize_w(LAST)
         multiply(1, LAST, HALVES)

@@ -38,7 +38,7 @@ ENDING = [FIRST_HALF, (HALF, HALF + QUARTER), (HALF + QUARTER, S)]
 
 PASS_0_SPLIT = 384
 PAIR_SPLIT = 256
-TAIL_SPLIT = 384
+TAIL_SPLIT = 320
 
 LAST_SPLIT = 96
 

@@ -38,7 +38,7 @@ ENDING = [FIRST_HALF, (HALF, HALF + QUARTER), (HALF + QUARTER, S)]
 
 PASS_0_SPLIT = 384
 PAIR_SPLIT = 256
-TAIL_SPLIT = 320
+TAIL_SPLIT = 352
 
 LAST_SPLIT = 96
 

from contextlib import ExitStack

import concourse.mybir as mybir
from concourse.masks import make_identity

K, T, D, S, V, N = 1024, 2048, 16, 512, 32, 512
FLOPS = 2 * K * N * S

F32 = mybir.dt.float32
BF16 = mybir.dt.bfloat16
U32 = mybir.dt.uint32
U16 = mybir.dt.uint16
U8 = mybir.dt.uint8
FP8X4 = mybir.dt.float8_e4m3fn_x4
SILU = mybir.ActivationFunctionType.Silu
COPY = mybir.ActivationFunctionType.Copy
AX = mybir.AxisListType.X
MAX = mybir.AluOpType.max
MULT = mybir.AluOpType.mult
ADD = mybir.AluOpType.add

P = 128
PACK = 4
K_PASS = P * PACK
PASSES = K // K_PASS
M_TILES = N // P
LAST = M_TILES - 1
STRIPE = 16
BANK = 512
BANK_BYTES = 4 * BANK
RUN = 4

HALF = S // 2
QUARTER = S // 4
FIRST_HALF, SECOND_HALF = (0, HALF), (HALF, S)
HALVES = [FIRST_HALF, SECOND_HALF]
ENDING = [FIRST_HALF, (HALF, HALF + QUARTER), (HALF + QUARTER, S)]

PASS_0_SPLIT = 384
PAIR_SPLIT = 256
TAIL_SPLIT = 352

LAST_SPLIT = 96

CODE_BYTES = 4 * P
LAST_GROUPED_OFFSET = 5120


def tile_picked_pool_lin_silu_sub_e_kernel(tc, xT, w, b, offs, out):
    nc = tc.nc
    with ExitStack() as ctx:
        lists = ctx.enter_context(tc.tile_pool(name="lists", bufs=1))
        keep = ctx.enter_context(tc.tile_pool(name="keep", bufs=1))
        late = ctx.enter_context(tc.tile_pool(name="late", bufs=1))
        psum = ctx.enter_context(tc.psum_pool(name="psum", bufs=1))

        b_rows = keep.tile([P, P], F32, name="b_rows")
        nc.gpsimd.memset(b_rows[:], 0.0)
        nc.scalar.dma_start(out=b_rows[0:M_TILES, :], in_=b.rearrange("(t p) o -> t (p o)", t=M_TILES))

        def pass_rows(tensor, a):
            return tensor[a * K_PASS : (a + 1) * K_PASS, :].rearrange("(p j) n -> p j n", j=PACK)

        planes = {}
        w_raw = {}

        def load_planes(a, j, count):
            table = keep.tile([P, count, T], F32, align_bytes=64, name=f"planes_{a}_{j}")
            nc.sync.dma_start(out=table[:], in_=pass_rows(xT, a)[:, j : j + count, :])
            for u in range(count):
                planes[(a, j + u)] = table[:, u, :]

        def load_w(a, m, tiles):
            raw = keep.tile([P, PACK, tiles * P], F32, align_bytes=64, name=f"raw_{a}_{m}", tag=f"raw_{a}_{m}")
            nc.sync.dma_start(out=raw[:], in_=pass_rows(w, a)[:, :, m * P : (m + tiles) * P])
            for u in range(tiles):
                w_raw[(a, m + u)] = (raw, u * P)

        offsets = lists.tile([P, S // STRIPE], U16, name="offsets")
        load_planes(0, 0, PACK)
        nc.sync.dma_start(offsets[:], offs)
        load_w(0, 0, M_TILES)
        load_planes(1, 0, 2)
        third_plane = keep.tile([P, 1, T], F32, align_bytes=64, name="third_plane", tag="third_plane")
        nc.sync.dma_start(out=third_plane[:], in_=pass_rows(xT, 1)[:, 2:3, :])
        planes[(1, 2)] = third_plane[:].rearrange("p u t -> p (u t)")
        last_plane = late.tile([P, T], F32, align_bytes=64, offset=0, name="last_plane")
        nc.sync.dma_start(out=last_plane[:], in_=pass_rows(xT, 1)[:, 3, :])
        planes[(1, 3)] = last_plane[:]
        for m in range(M_TILES):
            load_w(1, m, 1)

        warm = keep.tile([P, 1], F32, name="warm")
        warm_out = keep.tile([P, 1], F32, name="warm_out")
        nc.vector.memset(warm[:], 0.0)
        nc.scalar.activation(warm_out[:], warm[:], SILU)

        ident = keep.tile([P, P], F32, name="ident")
        bias = keep.tile([P, M_TILES], F32, align_bytes=64, name="bias", tag="third_plane")
        make_identity(nc, ident[:])
        b_cols = psum.tile([P, len(HALVES) * M_TILES * BANK], F32, offset=0, name="b_cols")
        nc.tensor.transpose(b_cols[:, 0:P], b_rows[:], ident[:])

        x_grouped = [keep.tile([P, S, PACK], BF16, align_bytes=64, name=f"xg_{a}") for a in range(PASSES)]
        x_codes = [keep.tile([P, S], U32, align_bytes=64, name=f"xc_{a}") for a in range(PASSES)]
        pass_0_x_scales = keep.tile([P, S], U8, align_bytes=64, name="xs_0")
        pass_1_x_scales = [
            keep.tile([P, HALF], U8, align_bytes=64, name="xs_1_first"),
            keep.tile([P, HALF], U8, align_bytes=64, name="xs_1_second", tag="raw_1_0"),
        ]

        def x_scales(a, n0, n1):
            return pass_0_x_scales[:, n0:n1] if a == 0 else pass_1_x_scales[n0 // HALF][:]

        def picked(a, j, n0, n1):
            return planes[(a, j)].indirect(offsets[:, n0 // STRIPE : n1 // STRIPE])

        def vector_gather(a, j, split):
            nc.vector.tensor_copy(out=x_grouped[a][:, 0:split, j], in_=picked(a, j, 0, split))

        def scalar_share(a, count, split):
            dense = keep.tile([P, count, S - split], F32, align_bytes=64, name=f"dense_{a}")
            for j in range(count):
                nc.scalar.activation(dense[:, j, :], picked(a, j, split, S), COPY)
            nc.scalar.copy(x_grouped[a][:, split:S, 0:count], dense[:].rearrange("p j n -> p n j"))

        def quantize_x(a, n0, n1):
            nc.vector.quantize_mx(
                out=x_codes[a][:, n0:n1].bitcast(FP8X4),
                scales=x_scales(a, n0, n1),
                in_=x_grouped[a][:, n0:n1, :].rearrange("p n j -> p (n j)"),
            )

        w_grouped, w_codes, w_scales = {}, {}, {}
        pass_0_grouped = keep.tile([P, N * PACK], BF16, align_bytes=64, name="wg_0")
        pass_0_codes = keep.tile([P, N], U32, align_bytes=64, name="wc_0")
        pass_0_scales = keep.tile([P, N], U8, align_bytes=64, name="ws_0")
        for m in range(M_TILES):
            w_grouped[(0, m)] = pass_0_grouped[:, m * P * PACK : (m + 1) * P * PACK]
            w_codes[(0, m)] = pass_0_codes[:, m * P : (m + 1) * P]
            w_scales[(0, m)] = pass_0_scales[:, m * P : (m + 1) * P]
        for m in range(M_TILES):
            if m == LAST:
                grouped = late.tile([P, P * PACK], BF16, align_bytes=64, offset=LAST_GROUPED_OFFSET, name=f"wg_1_{m}")
            else:
                grouped = keep.tile([P, P * PACK], BF16, align_bytes=64, name=f"wg_1_{m}", tag=f"wg_1_{m}")
            codes = late.tile([P, P], U32, align_bytes=64, offset=CODE_BYTES * m, name=f"wc_1_{m}")
            scales = keep.tile([P, P], U8, align_bytes=64, name=f"ws_1_{m}")
            w_grouped[(1, m)], w_codes[(1, m)], w_scales[(1, m)] = grouped[:], codes[:], scales[:]

        def interleave(copy, a, m, c0=0, c1=P):
            raw, first = w_raw[(a, m)]
            copy(
                w_grouped[(a, m)][:, c0 * PACK : c1 * PACK].rearrange("p (c i j) -> p c j i", i=RUN, j=PACK),
                raw[:, :, first + c0 : first + c1].rearrange("p j (c i) -> p c j i", i=RUN),
            )

        def quantize_w(m):
            nc.vector.quantize_mx(out=w_codes[(1, m)].bitcast(FP8X4), scales=w_scales[(1, m)], in_=w_grouped[(1, m)])

        sums = {}
        for m in range(M_TILES):
            for n0, n1 in HALVES:
                sums[(m, n0)] = psum.tile([P, HALF], F32, offset=BANK_BYTES * len(sums), name=f"sums_{m}_{n0}")

        def multiply(a, m, parts):
            for n0, n1 in parts:
                nc.tensor.matmul_mx(
                    out=sums[(m, n0)][:],
                    lhsT=w_codes[(a, m)].bitcast(FP8X4),
                    lhsT_scale=w_scales[(a, m)],
                    rhs=x_codes[a][:, n0:n1].bitcast(FP8X4),
                    rhs_scale=x_scales(a, n0, n1),
                    start=(a == 0),
                    stop=(a == PASSES - 1),
                )

        def activate(y, m, parts):
            for n0, n1 in parts:
                h0 = n0 // HALF * HALF
                nc.scalar.activation(
                    y[:, m, :][:, n0:n1], sums[(m, h0)][:, n0 - h0 : n1 - h0], SILU, bias=bias[:, m : m + 1]
                )

        def pool_max(pooled, y, m, parts):
            for n0, n1 in parts:
                nc.vector.tensor_reduce(
                    out=pooled[:, m, :][:, n0 // D : n1 // D],
                    in_=y[:, m, :][:, n0:n1].rearrange("p (v d) -> p v d", d=D),
                    axis=AX,
                    op=MAX,
                )

        out_view = out.rearrange("(t p) v -> p t v", p=P)

        for j in range(PACK):
            vector_gather(0, j, PASS_0_SPLIT)
        scalar_share(0, PACK, PASS_0_SPLIT)
        quantize_x(0, 0, S)
        for m in range(M_TILES):
            interleave(nc.scalar.copy, 0, m)
        for j in range(2):
            vector_gather(1, j, PAIR_SPLIT)
        scalar_share(1, 2, PAIR_SPLIT)
        nc.vector.quantize_mx(out=pass_0_codes[:].bitcast(FP8X4), scales=pass_0_scales[:], in_=pass_0_grouped[:])
        vector_gather(1, 2, TAIL_SPLIT)
        tail_dense = keep.tile([P, 2, S - TAIL_SPLIT], BF16, align_bytes=64, name="tail_dense")
        nc.scalar.activation(tail_dense[:, 0, :], picked(1, 2, TAIL_SPLIT, S), COPY)
        nc.scalar.copy(bias[:], b_cols[:, 0:M_TILES])
        for m in range(M_TILES):
            multiply(0, m, HALVES)

        vector_gather(1, 3, TAIL_SPLIT)
        nc.scalar.activation(tail_dense[:, 1, :], picked(1, 3, TAIL_SPLIT, S), COPY)
        nc.scalar.copy(x_grouped[1][:, TAIL_SPLIT:S, 2:PACK], tail_dense[:].rearrange("p e n -> p n e"))
        nc.gpsimd.tensor_scalar(
            w_grouped[(1, 0)].rearrange("p (c j) -> p c j", j=PACK),
            w_raw[(1, 0)][0][:].rearrange("p j c -> p c j"),
            1.0,
            0.0,
            op0=MULT,
            op1=ADD,
        )
        for m in range(1, LAST):
            interleave(nc.scalar.copy, 1, m)
        quantize_x(1, *FIRST_HALF)
        quantize_w(0)
        multiply(1, 0, [FIRST_HALF])
        quantize_x(1, *SECOND_HALF)
        multiply(1, 0, [SECOND_HALF])
        quantize_w(1)
        multiply(1, 1, HALVES)
        interleave(nc.vector.tensor_copy, 1, LAST, 0, LAST_SPLIT)
        quantize_w(2)
        multiply(1, 2, HALVES)
        y = keep.tile([P, M_TILES, S], F32, align_bytes=64, name="y", tag="wg_1_1")
        activate(y, 0, [FIRST_HALF])
        interleave(nc.scalar.copy, 1, LAST, LAST_SPLIT, P)
        activate(y, 0, [SECOND_HALF])
        for m in range(1, LAST):
            activate(y, m, HALVES)
        pooled = keep.tile([P, M_TILES, V], F32, align_bytes=64, name="pooled")
        pool_max(pooled, y, 0, [FIRST_HALF])
        quantize_w(LAST)
        multiply(1, LAST, HALVES)
        activate(y, LAST, ENDING)
        pool_max(pooled, y, 0, [SECOND_HALF])
        for m in range(1, LAST):
            pool_max(pooled, y, m, HALVES)
        nc.sync.dma_start(out=out_view[:, 0:LAST, :], in_=pooled[:, 0:LAST, :])
        pool_max(pooled, y, LAST, ENDING)
        nc.sync.dma_start(out=out_view[:, LAST, :], in_=pooled[:, LAST, :])
